import numpy as np
import ml_dtypes


def mxq(x, axis, fmt="e4m3"):
    dtype, down = {"e4m3": (ml_dtypes.float8_e4m3fn, 7), "e5m2": (ml_dtypes.float8_e5m2, 14)}[fmt]
    v = np.moveaxis(np.asarray(x, np.float32).astype(ml_dtypes.bfloat16).astype(np.float64), axis, -1)
    blocks = v.reshape(v.shape[:-1] + (-1, 32))
    amax = np.abs(blocks).max(-1, keepdims=True)
    byte = np.maximum(np.where(amax > 0, np.frexp(amax)[1] - 1 + 127, 0) - down, 1)
    scale = np.exp2(byte - 127.0)
    codes = (blocks / scale).astype(np.float32).astype(dtype).astype(np.float64)
    return np.moveaxis((codes * scale).reshape(v.shape), -1, axis)


WIDE = False


def mx_kscale(k):
    if not WIDE:
        return np.ones(k)
    levels = np.array([10, -10, 5, -5, 0])
    if k % 512:
        return np.exp2(np.random.permutation(np.resize(levels, k // 32))).repeat(32)
    a = np.empty((k // 512, 16))
    for p in range(k // 512):
        a[p, :8] = np.random.permutation(np.resize(levels, 8))
        for g in range(8):
            far = levels[np.abs(levels - a[p, g]) >= 10]
            a[p, g + 8] = far[np.random.randint(len(far))]
    return np.exp2(a.ravel()).repeat(32)


BF16 = ml_dtypes.bfloat16


def bf(x):
    return np.asarray(x, np.float32).astype(BF16)


def f64(x):
    return np.asarray(x).astype(np.float64)

def planes(Y):
    n, m = Y.shape
    b = f64(bf(Y)).reshape(n // 32, 32, m)
    amax = np.abs(b).max(1)
    byte = np.clip(np.where(amax > 0, np.frexp(amax)[1] - 1 + 127 - 7, 1), 1, 254)
    codes = (b * np.exp2(127.0 - byte)[:, None, :]).reshape(n, m).astype(np.float32).astype(ml_dtypes.float8_e4m3fn).view(np.uint8)
    words = codes.reshape(n // 512, 128, 4, m).transpose(0, 1, 3, 2)
    return np.ascontiguousarray(words), np.ascontiguousarray(byte.astype(np.uint8).reshape(n // 512, 16, m))


N, D, S, R = 1024, 512, 512, 1024
ALPHA = (0.1, 0.3, 0.6, 0.8)
A = len(ALPHA)
P = A * S


def relu(z):
    return np.maximum(z, 0.0)


def setup_inputs():
    s, t, u = mx_kscale(P), mx_kscale(R), mx_kscale(D)
    return {
        "x": bf(np.random.standard_normal((N, D)) * u),
        "mu": bf(np.random.standard_normal((N, P))),
        "gmu": bf((1.0 + 0.1 * np.random.standard_normal(P)) * s),
        "wr": bf(np.random.standard_normal((P, R)) / np.sqrt(P) / s[:, None]),
        "gr": bf(np.random.standard_normal(R) * t),
        "wphi": bf(np.random.standard_normal((R, S)) * 1.4 / np.sqrt(R) / t[:, None]),
        "wx": bf(np.random.standard_normal((D, S)) / np.sqrt(D) / u[:, None]),
    }


def core(x, mu, gmu, wr, gr, wphi, wx):
    x, mu, gmu, wr, gr, wphi, wx = f64(x), f64(mu), f64(gmu), f64(wr), f64(gr), f64(wphi), f64(wx)
    q = mu * gmu[None, :]
    r = gr[None, :] * relu(mxq(q, 1, "e4m3") @ mxq(wr, 0, "e4m3"))
    phi = relu((mxq(r, 1, "e4m3") @ mxq(wphi, 0, "e4m3")) + (mxq(x, 1, "e4m3") @ mxq(wx, 0, "e4m3")))
    blocks = []
    for a in range(A):
        old = mu[:, a * S:(a + 1) * S]
        blocks.append(ALPHA[a] * old + (1.0 - ALPHA[a]) * phi)
    return np.concatenate(blocks, axis=1)


def reference(x, mu, gmu, wr, gr, wphi, wx):
    R_out = core(x, mu, gmu, wr, gr, wphi, wx)
    words, scales = planes(R_out.T)
    return R_out, words, scales

@@ -1,0 +1,409 @@
+from contextlib import ExitStack
+
+import concourse.mybir as mybir
+from concourse.masks import make_identity
+
+N, D, S, R = 1024, 512, 512, 1024
+ALPHA = (0.1, 0.3, 0.6, 0.8)
+A = len(ALPHA)
+C = A * S
+FLOPS = 2 * N * (C * R + R * S + D * S)
+
+P = 128
+PACK = 4
+KP = P * PACK
+G1 = C // KP
+G2 = R // KP
+NT = N // P
+
+F32 = mybir.dt.float32
+BF16 = mybir.dt.bfloat16
+U32 = mybir.dt.uint32
+I32 = mybir.dt.int32
+U8 = mybir.dt.uint8
+FP8X4 = mybir.dt.float8_e4m3fn_x4
+ALU = mybir.AluOpType
+ACTF = mybir.ActivationFunctionType
+
+WR_ON = (76,)*8
+PE_TAGS = ("o_ps", "y_ps", "z_ps")
+ACT_CAST = tuple((i, b) for i in range(5) for b in range(2))
+
+
+def tile_statisticalrecurrentunitmultiscale_x1_kernel(
+    tc, x, mu, gmu, wr, gr, wphi, wx, out_0, out_1, out_2
+):
+    nc = tc.nc
+    with ExitStack() as ctx:
+        ctx.enter_context(nc.allow_non_contiguous_dma(reason="two small gate vectors"))
+        keep = ctx.enter_context(tc.tile_pool(name="keep", bufs=1))
+        work = ctx.enter_context(tc.tile_pool(name="work", bufs=2))
+        psum = ctx.enter_context(tc.psum_pool(name="psum", bufs=2))
+
+        gmu_t = keep.tile([P, G1, 2, 2], BF16, name="gmu_t")
+        gr_t = keep.tile([P, G2, PACK], BF16, name="gr_t")
+        mu_sb = [keep.tile([P, C], BF16, name=f"mu_{i}", align_bytes=64) for i in range(NT)]
+        x_sb = keep.tile([P, NT, D], BF16, name="x_sb", align_bytes=64)
+        wr_raw = [keep.tile([P, PACK, R], BF16, name=f"wr_raw_{g}", align_bytes=64) for g in range(G1)]
+        wx_raw = keep.tile([P, PACK, S], BF16, name="wx_raw", align_bytes=64)
+        wphi_raw = [keep.tile([P, PACK, S], BF16, name=f"wphi_raw_{g}", align_bytes=64) for g in range(G2)]
+
+        def load_mu(i):
+            nc.sync.dma_start(out=mu_sb[i][:], in_=mu[P * i : P * (i + 1), :])
+
+        def load_wr(g, h):
+            src = wr[KP * g : KP * (g + 1), :].rearrange("(p j) c -> p j c", j=PACK)
+            nc.sync.dma_start(out=wr_raw[g][:, :, KP * h : KP * (h + 1)], in_=src[:, :, KP * h : KP * (h + 1)])
+
+        gates = nc.scalar
+        for g in range(G1):
+            load_wr(g, 0)
+            if g == 0:
+                gates.dma_start(out=gmu_t[:], in_=gmu.rearrange("(g p u e) -> p g u e", p=P, u=2, e=2))
+            if g == 2:
+                load_mu(0)
+        gates.dma_start(out=gr_t[:], in_=gr.rearrange("(g p t) -> p g t", p=P, t=PACK))
+        load_mu(1)
+        for g in range(G1):
+            load_wr(g, 1)
+            if g == 1:
+                load_mu(2)
+        nc.sync.dma_start(out=x_sb[:], in_=x.rearrange("(i p) d -> p i d", p=P))
+        nc.sync.dma_start(out=wx_raw[:], in_=wx.rearrange("(p j) c -> p j c", j=PACK))
+        for g in range(G2):
+            nc.sync.dma_start(out=wphi_raw[g][:], in_=wphi[KP * g : KP * (g + 1), :].rearrange("(p j) c -> p j c", j=PACK))
+        for i in range(3, NT):
+            load_mu(i)
+
+        ident = keep.tile([P, P], F32, name="ident")
+        make_identity(nc, ident[:])
+        ident_bf = keep.tile([P, P], BF16, name="ident_bf")
+        nc.vector.tensor_copy(out=ident_bf[:], in_=ident[:])
+        warm = keep.tile([P, 1], F32, name="warm")
+        nc.vector.memset(warm[:], 0.0)
+        nc.scalar.activation(out=warm[:], in_=warm[:], func=ACTF.Relu)
+
+        codes, scales, grouped = {}, {}, {}
+
+        def copy_on(engine, out, in_):
+            if engine == "act":
+                nc.scalar.copy(out=out, in_=in_)
+            else:
+                nc.vector.tensor_copy(out=out, in_=in_)
+
+        def wr_copy(g, h, engine):
+            if engine in ("pa", "pd"):
+                pe_copy(g, h, ("act", "act") if engine == "pa" else ("act", "dve"))
+                return
+            if engine not in ("act", "dve"):
+                gt = work.tile([P, PACK, P, PACK], BF16, name="w_grouped", tag="w_grouped", bufs=4, align_bytes=64)
+                grouped["wr", g, h] = gt
+                raw = wr_raw[g][:, :, KP * h : KP * (h + 1)].rearrange("p j (m t) -> p m t j", t=PACK)
+                for e, ms in (("act", slice(0, engine)), ("dve", slice(engine, P))):
+                    copy_on(e, gt[:, :, ms].rearrange("p t m j -> p m t j"), raw[:, ms])
+                return
+            gt = work.tile([P, PACK, P, PACK], BF16, name="w_grouped", tag="w_grouped", bufs=4, align_bytes=64)
+            grouped["wr", g, h] = gt
+            copy_on(
+                engine,
+                gt[:].rearrange("p t m j -> p m t j"),
+                wr_raw[g][:, :, KP * h : KP * (h + 1)].rearrange("p j (m t) -> p m t j", t=PACK),
+            )
+
+        def pe_copy(g, h, engine):
+            gt = work.tile([P, PACK, P, PACK], BF16, name="w_grouped", tag="w_grouped", bufs=4, align_bytes=64)
+            grouped["wr", g, h] = gt
+            raw = wr_raw[g][:, :, KP * h : KP * (h + 1)].rearrange("p j (m t) -> p j m t", t=PACK)
+            for b in range(2):
+                ts = slice(2 * b, 2 * b + 2)
+                ps = psum.tile([P, 2, P, PACK], BF16, name="c_ps", tag=PE_TAGS[(4 * g + 2 * h + b) % len(PE_TAGS)], bufs=2)
+                for j in range(PACK):
+                    nc.tensor.matmul(
+                        ps[:, :, :, j].rearrange("p t m -> p m t"), lhsT=ident_bf[:], rhs=raw[:, j, :, ts], start=True, stop=True
+                    )
+                copy_on(engine[b], gt[:, ts].rearrange("p t m j -> p (t m j)"), ps[:].rearrange("p t m j -> p (t m j)"))
+
+        def w_copy(key, raw, engine):
+            gt = work.tile([P, S, PACK], BF16, name="w_grouped", tag="w_grouped", bufs=4, align_bytes=64)
+            grouped[key] = gt
+            copy_on(engine, gt[:], raw[:].rearrange("p j c -> p c j"))
+
+        def w_quant(key):
+            nm = "_".join(str(k) for k in key)
+            ct = keep.tile([P, KP], U32, name="wc_" + nm, align_bytes=64)
+            st = keep.tile([P, KP], U8, name="ws_" + nm, align_bytes=64)
+            codes[key], scales[key] = ct, st
+            src = grouped[key][:]
+            src = src.rearrange("p t m j -> p (t m j)") if key[0] == "wr" else src.rearrange("p c j -> p (c j)")
+            nc.vector.quantize_mx(out=ct[:].bitcast(FP8X4), scales=st[:], in_=src)
+
+        q_ps, q_gr, q_codes, q_scales = {}, {}, {}, {}
+
+        def q_turn(i):
+            words = mu_sb[i][:].bitcast(F32)
+            for b in range(2):
+                ps = psum.tile([P, 2, 2, P], F32, name="q_ps", tag="q_ps", bufs=2)
+                q_ps[i, b] = ps
+                for k in range(2):
+                    g = 2 * b + k
+                    for u in range(2):
+                        nc.tensor.transpose(ps[:, u, k, :], words[:, 256 * g + u : 256 * (g + 1) : 2], ident[:])
+
+        def q_mul(i):
+            qg = work.tile([P, G1, P, 2, 2], BF16, name="q_gr", tag="q_gr", bufs=2, align_bytes=64)
+            q_gr[i] = qg
+            for b in range(2):
+                src = q_ps[i, b][:].rearrange("p u g r -> p u (g r)").bitcast(BF16)
+                nc.vector.tensor_tensor(
+                    out=qg[:, 2 * b : 2 * b + 2],
+                    in0=src.rearrange("p u (g r e) -> p g r u e", g=2, e=2),
+                    in1=gmu_t[:, 2 * b : 2 * b + 2].unsqueeze(2).to_broadcast([P, 2, P, 2, 2]),
+                    op=ALU.mult,
+                )
+
+        def q_quant(i):
+            ct = work.tile([P, G1, P], U32, name="q_codes", tag="q_codes", bufs=4, align_bytes=64)
+            st = work.tile([P, G1, P], U8, name="q_scales", tag="q_scales", bufs=4, align_bytes=64)
+            q_codes[i], q_scales[i] = ct, st
+            nc.vector.quantize_mx(
+                out=ct[:].rearrange("p g n -> p (g n)").bitcast(FP8X4),
+                scales=st[:].rearrange("p g n -> p (g n)"),
+                in_=q_gr[i][:].rearrange("p g n u e -> p (g n u e)"),
+            )
+
+        x_gr = keep.tile([P, N, PACK], BF16, name="x_gr", align_bytes=64)
+        x_codes = keep.tile([P, N], U32, name="x_codes", align_bytes=64)
+        x_scales = keep.tile([P, N], U8, name="x_scales", align_bytes=64)
+        x_ps = {}
+
+        def x_turn(j):
+            ps = psum.tile([P, 2, 2, P], F32, name="o_ps", tag="o_ps", bufs=2)
+            x_ps[j] = ps
+            for k in range(2):
+                words = x_sb[:, 2 * j + k, :].bitcast(F32)
+                for u in range(2):
+                    nc.tensor.transpose(ps[:, u, k, :], words[:, u : 256 : 2], ident[:])
+
+        def x_copy(j, engine):
+            copy_on(
+                engine,
+                x_gr[:, 256 * j : 256 * (j + 1), :].rearrange("p n t -> p (n t)").bitcast(F32).rearrange("p (n u) -> p n u", u=2),
+                x_ps[j][:].rearrange("p u k r -> p (k r) u"),
+            )
+
+        def x_quant(h):
+            w = N // 2
+            nc.vector.quantize_mx(
+                out=x_codes[:, w * h : w * (h + 1)].bitcast(FP8X4),
+                scales=x_scales[:, w * h : w * (h + 1)],
+                in_=x_gr[:, w * h : w * (h + 1), :].rearrange("p n t -> p (n t)"),
+            )
+
+        z_ps, r_gr, r_codes, r_scales = {}, {}, {}, {}
+
+        def s1(i, h):
+            ps = psum.tile([P, PACK, P], F32, name="z_ps", tag="z_ps", bufs=2)
+            z_ps[i, h] = ps
+            for t in range(PACK):
+                cols = slice(P * t, P * (t + 1))
+                for g in range(G1):
+                    nc.tensor.matmul_mx(
+                        out=ps[:, t, :],
+                        lhsT=codes["wr", g, h][:, cols].bitcast(FP8X4),
+                        lhsT_scale=scales["wr", g, h][:, cols],
+                        rhs=q_codes[i][:, g, :].bitcast(FP8X4),
+                        rhs_scale=q_scales[i][:, g, :],
+                        start=(g == 0),
+                        stop=(g == G1 - 1),
+                    )
+
+        def r_mul(i, h):
+            if h == 0:
+                r_gr[i] = work.tile([P, G2, P, PACK], BF16, name="r_gr", tag="r_gr", bufs=4, align_bytes=64)
+            nc.vector.scalar_tensor_tensor(
+                out=r_gr[i][:, h],
+                in0=z_ps[i, h][:].rearrange("p t n -> p n t"),
+                scalar=0.0,
+                in1=gr_t[:, h, :].unsqueeze(1).to_broadcast([P, P, PACK]),
+                op0=ALU.max,
+                op1=ALU.mult,
+            )
+
+        def r_quant(i):
+            ct = work.tile([P, G2, P], U32, name="r_codes", tag="r_codes", bufs=4, align_bytes=64)
+            st = work.tile([P, G2, P], U8, name="r_scales", tag="r_scales", bufs=4, align_bytes=64)
+            r_codes[i], r_scales[i] = ct, st
+            nc.vector.quantize_mx(
+                out=ct[:].rearrange("p g n -> p (g n)").bitcast(FP8X4),
+                scales=st[:].rearrange("p g n -> p (g n)"),
+                in_=r_gr[i][:].rearrange("p g n t -> p (g n t)"),
+            )
+
+        y_ps, part, res = {}, {}, {}
+
+        def s2(i):
+            ps = psum.tile([P, S], F32, name="y_ps", tag="y_ps", bufs=2)
+            y_ps[i] = ps
+            rows = slice(P * i, P * (i + 1))
+            nc.tensor.matmul_mx(
+                out=ps[:],
+                lhsT=x_codes[:, rows].bitcast(FP8X4),
+                lhsT_scale=x_scales[:, rows],
+                rhs=codes["wx",][:].bitcast(FP8X4),
+                rhs_scale=scales["wx",][:],
+                start=True,
+                stop=False,
+            )
+            for g in range(G2):
+                nc.tensor.matmul_mx(
+                    out=ps[:],
+                    lhsT=r_codes[i][:, g, :].bitcast(FP8X4),
+                    lhsT_scale=r_scales[i][:, g, :],
+                    rhs=codes["wphi", g][:].bitcast(FP8X4),
+                    rhs_scale=scales["wphi", g][:],
+                    start=False,
+                    stop=(g == G2 - 1),
+                )
+
+        def phi(i, a):
+            pt = work.tile([P, S], F32, name="part", tag="part", bufs=6)
+            part[i, a] = pt
+            nc.scalar.activation(out=pt[:], in_=y_ps[i][:], func=ACTF.Relu, scale=1.0 - ALPHA[a])
+
+        def mix(i, a):
+            if a == 0:
+                res[i] = work.tile([P, C], F32, name="res", tag="res", bufs=3)
+            cols = slice(S * a, S * (a + 1))
+            nc.vector.scalar_tensor_tensor(
+                out=res[i][:, cols],
+                in0=mu_sb[i][:, cols],
+                scalar=ALPHA[a],
+                in1=part[i, a][:],
+                op0=ALU.mult,
+                op1=ALU.add,
+            )
+
+        def res_store(i, a0=0, a1=A):
+            cols = slice(S * a0, S * a1)
+            nc.sync.dma_start(out=out_0[P * i : P * (i + 1), cols], in_=res[i][:, cols])
+
+        o_bf, o_ps, o_gr, o_codes, o_scales = {}, {}, {}, {}, {}
+
+        def o_cast(i, engine, w0, w1):
+            if i not in o_bf:
+                o_bf[i] = work.tile([P, 2, C // 4, 2], BF16, name="o_bf", tag="o_bf", bufs=2, align_bytes=64)
+            copy_on(
+                engine,
+                o_bf[i][:, :, w0:w1],
+                res[i][:, 4 * w0 : 4 * w1].rearrange("p (w u e) -> p u w e", u=2, e=2),
+            )
+
+        def o_turn(i, b0=0, b1=2):
+            for b in range(b0, b1):
+                ps = psum.tile([P, 2, 2, P], F32, name="o_ps", tag="o_ps", bufs=2)
+                o_ps[i, b] = ps
+                for u in range(2):
+                    words = o_bf[i][:, u].rearrange("p w e -> p (w e)").bitcast(F32)
+                    for k in range(2):
+                        g = 2 * b + k
+                        nc.tensor.transpose(ps[:, u, k, :], words[:, P * g : P * (g + 1)], ident[:])
+
+        def o_copy(i, b, engine="act"):
+            if b == 0:
+                o_gr[i] = work.tile([P, G1, P, PACK], BF16, name="o_gr", tag="o_gr", bufs=2, align_bytes=64)
+            copy_on(
+                engine,
+                o_gr[i][:, 2 * b : 2 * b + 2].rearrange("p g n t -> p (g n t)").bitcast(F32).rearrange("p (n u) -> p n u", u=2),
+                o_ps[i, b][:].rearrange("p u k r -> p (k r) u"),
+            )
+
+        def o_quant(i, b0=0, b1=2):
+            if i not in o_codes:
+                o_codes[i] = work.tile([P, G1, P], U32, name="o_codes", tag="o_codes", bufs=3, align_bytes=64)
+                o_scales[i] = work.tile([P, G1, P], U8, name="o_scales", tag="o_scales", bufs=3, align_bytes=64)
+            gs = slice(2 * b0, 2 * b1)
+            nc.vector.quantize_mx(
+                out=o_codes[i][:, gs].rearrange("p g n -> p (g n)").bitcast(FP8X4),
+                scales=o_scales[i][:, gs].rearrange("p g n -> p (g n)"),
+                in_=o_gr[i][:, gs].rearrange("p g n t -> p (g n t)"),
+            )
+
+        def o_store(i, b0=0, b1=2):
+            gs = slice(2 * b0, 2 * b1)
+            words = out_1.rearrange("g p m t -> p g (m t)")
+            nc.sync.dma_start(
+                out=words[:, gs, KP * i : KP * (i + 1)].bitcast(I32), in_=o_codes[i][:, gs].bitcast(I32)
+            )
+            rows = out_2.rearrange("g (q r) m -> q r g m", r=4)
+            for q in range(4):
+                nc.sync.dma_start(
+                    out=rows[q, :, gs, P * i : P * (i + 1)].bitcast(I32),
+                    in_=o_scales[i][32 * q : 32 * q + 4, gs].bitcast(I32),
+                )
+
+        def make_wr(h):
+            for g in range(G1):
+                wr_copy(g, h, WR_ON[4 * h + g])
+                w_quant(("wr", g, h))
+
+        def make_q(i):
+            q_turn(i)
+            q_mul(i)
+            q_quant(i)
+
+        def make_r(i):
+            s1(i, 0)
+            s1(i, 1)
+            r_mul(i, 0)
+            r_mul(i, 1)
+            r_quant(i)
+
+        def make_out(i):
+            last = i >= NT - 1
+            for b in range(2):
+                for a in (2 * b, 2 * b + 1):
+                    mix(i, a)
+                    if last:
+                        o_cast(i, "dve", 128 * a, 128 * (a + 1))
+                if last:
+                    res_store(i, 2 * b, 2 * b + 2)
+                else:
+                    o_cast(i, "act" if (i, b) in ACT_CAST else "dve", 256 * b, 256 * (b + 1))
+                o_turn(i, b, b + 1)
+                o_copy(i, b)
+                if last:
+                    o_quant(i, b, b + 1)
+                    o_store(i, b, b + 1)
+            if not last:
+                res_store(i)
+                o_quant(i)
+                o_store(i)
+
+        for i in range(NT + 3):
+            if i == 0:
+                make_wr(0)
+            if i < NT:
+                make_q(i)
+            if i == 0:
+                make_wr(1)
+            if i == 0:
+                for j in range(4):
+                    x_turn(j)
+                    x_copy(j, "act")
+                w_copy(("wx",), wx_raw, "dve")
+                x_quant(0)
+                w_quant(("wx",))
+                w_copy(("wphi", 0), wphi_raw[0], "act")
+                x_quant(1)
+                w_copy(("wphi", 1), wphi_raw[1], "act")
+                w_quant(("wphi", 0))
+                w_quant(("wphi", 1))
+            k = i - 1
+            if 0 <= k < NT:
+                make_r(k)
+            k = i - 3
+            if 0 <= k < NT:
+                s2(k)
+                for a in range(A):
+                    phi(k, a)
+                make_out(k)

@@ -25,10 +25,6 @@ FP8X4 = mybir.dt.float8_e4m3fn_x4
 ALU = mybir.AluOpType
 ACTF = mybir.ActivationFunctionType
 
-WR_ON = (76,)*8
-PE_TAGS = ("o_ps", "y_ps", "z_ps")
-ACT_CAST = tuple((i, b) for i in range(5) for b in range(2))
-
 
 def tile_statisticalrecurrentunitmultiscale_x1_kernel(
     tc, x, mu, gmu, wr, gr, wphi, wx, out_0, out_1, out_2
@@ -40,11 +36,13 @@ def tile_statisticalrecurrentunitmultiscale_x1_kernel(
         work = ctx.enter_context(tc.tile_pool(name="work", bufs=2))
         psum = ctx.enter_context(tc.psum_pool(name="psum", bufs=2))
 
+        ctx.enter_context(tc.manual_schedule())
+
         gmu_t = keep.tile([P, G1, 2, 2], BF16, name="gmu_t")
         gr_t = keep.tile([P, G2, PACK], BF16, name="gr_t")
         mu_sb = [keep.tile([P, C], BF16, name=f"mu_{i}", align_bytes=64) for i in range(NT)]
         x_sb = keep.tile([P, NT, D], BF16, name="x_sb", align_bytes=64)
-        wr_raw = [keep.tile([P, PACK, R], BF16, name=f"wr_raw_{g}", align_bytes=64) for g in range(G1)]
+        wr_raw = [work.tile([P, PACK, R], BF16, name=f"wr_raw_{g}", tag="big", bufs=4, align_bytes=64) for g in range(G1)]
         wx_raw = keep.tile([P, PACK, S], BF16, name="wx_raw", align_bytes=64)
         wphi_raw = [keep.tile([P, PACK, S], BF16, name=f"wphi_raw_{g}", align_bytes=64) for g in range(G2)]
 
@@ -56,29 +54,42 @@ def tile_statisticalrecurrentunitmultiscale_x1_kernel(
             nc.sync.dma_start(out=wr_raw[g][:, :, KP * h : KP * (h + 1)], in_=src[:, :, KP * h : KP * (h + 1)])
 
         gates = nc.scalar
-        for g in range(G1):
-            load_wr(g, 0)
-            if g == 0:
-                gates.dma_start(out=gmu_t[:], in_=gmu.rearrange("(g p u e) -> p g u e", p=P, u=2, e=2))
-            if g == 2:
-                load_mu(0)
+        def load_x():
+            nc.sync.dma_start(out=x_sb[:], in_=x.rearrange("(i p) d -> p i d", p=P))
+
+        def load_wx():
+            nc.sync.dma_start(out=wx_raw[:], in_=wx.rearrange("(p j) c -> p j c", j=PACK))
+
+        def load_wphi(g):
+            nc.sync.dma_start(
+                out=wphi_raw[g][:], in_=wphi[KP * g : KP * (g + 1), :].rearrange("(p j) c -> p j c", j=PACK)
+            )
+
+        gates.dma_start(out=gmu_t[:], in_=gmu.rearrange("(g p u e) -> p g u e", p=P, u=2, e=2))
         gates.dma_start(out=gr_t[:], in_=gr.rearrange("(g p t) -> p g t", p=P, t=PACK))
         load_mu(1)
-        for g in range(G1):
-            load_wr(g, 1)
-            if g == 1:
-                load_mu(2)
-        nc.sync.dma_start(out=x_sb[:], in_=x.rearrange("(i p) d -> p i d", p=P))
-        nc.sync.dma_start(out=wx_raw[:], in_=wx.rearrange("(p j) c -> p j c", j=PACK))
-        for g in range(G2):
-            nc.sync.dma_start(out=wphi_raw[g][:], in_=wphi[KP * g : KP * (g + 1), :].rearrange("(p j) c -> p j c", j=PACK))
-        for i in range(3, NT):
-            load_mu(i)
+        load_wr(3, 0)
+        load_wr(1, 1)
+        load_wr(2, 0)
+        load_mu(0)
+        load_wr(1, 0)
+        load_mu(2)
+        load_wr(0, 0)
+        load_wr(2, 1)
+        load_mu(3)
+        load_wr(0, 1)
+        load_wr(3, 1)
+        load_wphi(1)
+        load_wphi(0)
+        load_x()
+        load_mu(4)
+        load_wx()
+        load_mu(5)
+        load_mu(7)
+        load_mu(6)
 
         ident = keep.tile([P, P], F32, name="ident")
         make_identity(nc, ident[:])
-        ident_bf = keep.tile([P, P], BF16, name="ident_bf")
-        nc.vector.tensor_copy(out=ident_bf[:], in_=ident[:])
         warm = keep.tile([P, 1], F32, name="warm")
         nc.vector.memset(warm[:], 0.0)
         nc.scalar.activation(out=warm[:], in_=warm[:], func=ACTF.Relu)
@@ -91,37 +102,13 @@ def tile_statisticalrecurrentunitmultiscale_x1_kernel(
             else:
                 nc.vector.tensor_copy(out=out, in_=in_)
 
-        def wr_copy(g, h, engine):
-            if engine in ("pa", "pd"):
-                pe_copy(g, h, ("act", "act") if engine == "pa" else ("act", "dve"))
-                return
-            if engine not in ("act", "dve"):
-                gt = work.tile([P, PACK, P, PACK], BF16, name="w_grouped", tag="w_grouped", bufs=4, align_bytes=64)
-                grouped["wr", g, h] = gt
-                raw = wr_raw[g][:, :, KP * h : KP * (h + 1)].rearrange("p j (m t) -> p m t j", t=PACK)
-                for e, ms in (("act", slice(0, engine)), ("dve", slice(engine, P))):
-                    copy_on(e, gt[:, :, ms].rearrange("p t m j -> p m t j"), raw[:, ms])
-                return
-            gt = work.tile([P, PACK, P, PACK], BF16, name="w_grouped", tag="w_grouped", bufs=4, align_bytes=64)
-            grouped["wr", g, h] = gt
+        def wr_copy(g, h, engine, m0, m1):
+            if ("wr", g, h) not in grouped:
+                grouped["wr", g, h] = work.tile([P, PACK, P, PACK], BF16, name="w_grouped", tag="w_grouped", bufs=4, align_bytes=64)
+            raw = wr_raw[g][:, :, KP * h : KP * (h + 1)].rearrange("p j (m t) -> p m t j", t=PACK)
             copy_on(
-                engine,
-                gt[:].rearrange("p t m j -> p m t j"),
-                wr_raw[g][:, :, KP * h : KP * (h + 1)].rearrange("p j (m t) -> p m t j", t=PACK),
+                engine, grouped["wr", g, h][:, :, m0:m1].rearrange("p t m j -> p m t j"), raw[:, m0:m1]
             )
-
-        def pe_copy(g, h, engine):
-            gt = work.tile([P, PACK, P, PACK], BF16, name="w_grouped", tag="w_grouped", bufs=4, align_bytes=64)
-            grouped["wr", g, h] = gt
-            raw = wr_raw[g][:, :, KP * h : KP * (h + 1)].rearrange("p j (m t) -> p j m t", t=PACK)
-            for b in range(2):
-                ts = slice(2 * b, 2 * b + 2)
-                ps = psum.tile([P, 2, P, PACK], BF16, name="c_ps", tag=PE_TAGS[(4 * g + 2 * h + b) % len(PE_TAGS)], bufs=2)
-                for j in range(PACK):
-                    nc.tensor.matmul(
-                        ps[:, :, :, j].rearrange("p t m -> p m t"), lhsT=ident_bf[:], rhs=raw[:, j, :, ts], start=True, stop=True
-                    )
-                copy_on(engine[b], gt[:, ts].rearrange("p t m j -> p (t m j)"), ps[:].rearrange("p t m j -> p (t m j)"))
 
         def w_copy(key, raw, engine):
             gt = work.tile([P, S, PACK], BF16, name="w_grouped", tag="w_grouped", bufs=4, align_bytes=64)
@@ -139,31 +126,29 @@ def tile_statisticalrecurrentunitmultiscale_x1_kernel(
 
         q_ps, q_gr, q_codes, q_scales = {}, {}, {}, {}
 
-        def q_turn(i):
+        def q_turn(i, b):
             words = mu_sb[i][:].bitcast(F32)
-            for b in range(2):
-                ps = psum.tile([P, 2, 2, P], F32, name="q_ps", tag="q_ps", bufs=2)
-                q_ps[i, b] = ps
-                for k in range(2):
-                    g = 2 * b + k
-                    for u in range(2):
-                        nc.tensor.transpose(ps[:, u, k, :], words[:, 256 * g + u : 256 * (g + 1) : 2], ident[:])
+            ps = psum.tile([P, 2, 2, P], F32, name="q_ps", tag="q_ps", bufs=2)
+            q_ps[i, b] = ps
+            for k in range(2):
+                g = 2 * b + k
+                for u in range(2):
+                    nc.tensor.transpose(ps[:, u, k, :], words[:, 256 * g + u : 256 * (g + 1) : 2], ident[:])
 
-        def q_mul(i):
-            qg = work.tile([P, G1, P, 2, 2], BF16, name="q_gr", tag="q_gr", bufs=2, align_bytes=64)
-            q_gr[i] = qg
-            for b in range(2):
-                src = q_ps[i, b][:].rearrange("p u g r -> p u (g r)").bitcast(BF16)
-                nc.vector.tensor_tensor(
-                    out=qg[:, 2 * b : 2 * b + 2],
-                    in0=src.rearrange("p u (g r e) -> p g r u e", g=2, e=2),
-                    in1=gmu_t[:, 2 * b : 2 * b + 2].unsqueeze(2).to_broadcast([P, 2, P, 2, 2]),
-                    op=ALU.mult,
-                )
+        def q_mul(i, b):
+            if i not in q_gr:
+                q_gr[i] = work.tile([P, G1, P, 2, 2], BF16, name="q_gr", tag="q_gr", bufs=2, align_bytes=64)
+            src = q_ps[i, b][:].rearrange("p u g r -> p u (g r)").bitcast(BF16)
+            nc.vector.tensor_tensor(
+                out=q_gr[i][:, 2 * b : 2 * b + 2],
+                in0=src.rearrange("p u (g r e) -> p g r u e", g=2, e=2),
+                in1=gmu_t[:, 2 * b : 2 * b + 2].unsqueeze(2).to_broadcast([P, 2, P, 2, 2]),
+                op=ALU.mult,
+            )
 
         def q_quant(i):
-            ct = work.tile([P, G1, P], U32, name="q_codes", tag="q_codes", bufs=4, align_bytes=64)
-            st = work.tile([P, G1, P], U8, name="q_scales", tag="q_scales", bufs=4, align_bytes=64)
+            ct = work.tile([P, G1, P], U32, name="q_codes", tag="q_codes", bufs=8, align_bytes=64)
+            st = work.tile([P, G1, P], U8, name="q_scales", tag="q_scales", bufs=8, align_bytes=64)
             q_codes[i], q_scales[i] = ct, st
             nc.vector.quantize_mx(
                 out=ct[:].rearrange("p g n -> p (g n)").bitcast(FP8X4),
@@ -218,8 +203,8 @@ def tile_statisticalrecurrentunitmultiscale_x1_kernel(
                     )
 
         def r_mul(i, h):
-            if h == 0:
-                r_gr[i] = work.tile([P, G2, P, PACK], BF16, name="r_gr", tag="r_gr", bufs=4, align_bytes=64)
+            if i not in r_gr:
+                r_gr[i] = work.tile([P, G2, P, PACK], BF16, name="r_gr", tag="r_gr", bufs=3, align_bytes=64)
             nc.vector.scalar_tensor_tensor(
                 out=r_gr[i][:, h],
                 in0=z_ps[i, h][:].rearrange("p t n -> p n t"),
@@ -271,8 +256,8 @@ def tile_statisticalrecurrentunitmultiscale_x1_kernel(
             nc.scalar.activation(out=pt[:], in_=y_ps[i][:], func=ACTF.Relu, scale=1.0 - ALPHA[a])
 
         def mix(i, a):
-            if a == 0:
-                res[i] = work.tile([P, C], F32, name="res", tag="res", bufs=3)
+            if i not in res:
+                res[i] = work.tile([P, C], F32, name="res", tag="big", bufs=4, align_bytes=64)
             cols = slice(S * a, S * (a + 1))
             nc.vector.scalar_tensor_tensor(
                 out=res[i][:, cols],
@@ -309,7 +294,7 @@ def tile_statisticalrecurrentunitmultiscale_x1_kernel(
                         nc.tensor.transpose(ps[:, u, k, :], words[:, P * g : P * (g + 1)], ident[:])
 
         def o_copy(i, b, engine="act"):
-            if b == 0:
+            if i not in o_gr:
                 o_gr[i] = work.tile([P, G1, P, PACK], BF16, name="o_gr", tag="o_gr", bufs=2, align_bytes=64)
             copy_on(
                 engine,
@@ -317,16 +302,17 @@ def tile_statisticalrecurrentunitmultiscale_x1_kernel(
                 o_ps[i, b][:].rearrange("p u k r -> p (k r) u"),
             )
 
+        scales_all = keep.tile([P, G1, N], U8, name="o_scales", align_bytes=64)
+
         def o_quant(i, b0=0, b1=2):
             if i not in o_codes:
                 o_codes[i] = work.tile([P, G1, P], U32, name="o_codes", tag="o_codes", bufs=3, align_bytes=64)
-                o_scales[i] = work.tile([P, G1, P], U8, name="o_scales", tag="o_scales", bufs=3, align_bytes=64)
-            gs = slice(2 * b0, 2 * b1)
-            nc.vector.quantize_mx(
-                out=o_codes[i][:, gs].rearrange("p g n -> p (g n)").bitcast(FP8X4),
-                scales=o_scales[i][:, gs].rearrange("p g n -> p (g n)"),
-                in_=o_gr[i][:, gs].rearrange("p g n t -> p (g n t)"),
-            )
+            for g in range(2 * b0, 2 * b1):
+                nc.vector.quantize_mx(
+                    out=o_codes[i][:, g, :].bitcast(FP8X4),
+                    scales=scales_all[:, g, P * i : P * (i + 1)],
+                    in_=o_gr[i][:, g].rearrange("p n t -> p (n t)"),
+                )
 
         def o_store(i, b0=0, b1=2):
             gs = slice(2 * b0, 2 * b1)
@@ -334,76 +320,281 @@ def tile_statisticalrecurrentunitmultiscale_x1_kernel(
             nc.sync.dma_start(
                 out=words[:, gs, KP * i : KP * (i + 1)].bitcast(I32), in_=o_codes[i][:, gs].bitcast(I32)
             )
+
+        def scale_store(i0, i1):
             rows = out_2.rearrange("g (q r) m -> q r g m", r=4)
             for q in range(4):
                 nc.sync.dma_start(
-                    out=rows[q, :, gs, P * i : P * (i + 1)].bitcast(I32),
-                    in_=o_scales[i][32 * q : 32 * q + 4, gs].bitcast(I32),
+                    out=rows[q, :, :, P * i0 : P * i1].bitcast(I32),
+                    in_=scales_all[32 * q : 32 * q + 4, :, P * i0 : P * i1].bitcast(I32),
                 )
 
-        def make_wr(h):
-            for g in range(G1):
-                wr_copy(g, h, WR_ON[4 * h + g])
-                w_quant(("wr", g, h))
-
-        def make_q(i):
-            q_turn(i)
-            q_mul(i)
-            q_quant(i)
-
-        def make_r(i):
-            s1(i, 0)
-            s1(i, 1)
-            r_mul(i, 0)
-            r_mul(i, 1)
-            r_quant(i)
-
-        def make_out(i):
-            last = i >= NT - 1
-            for b in range(2):
-                for a in (2 * b, 2 * b + 1):
-                    mix(i, a)
-                    if last:
-                        o_cast(i, "dve", 128 * a, 128 * (a + 1))
-                if last:
-                    res_store(i, 2 * b, 2 * b + 2)
-                else:
-                    o_cast(i, "act" if (i, b) in ACT_CAST else "dve", 256 * b, 256 * (b + 1))
-                o_turn(i, b, b + 1)
-                o_copy(i, b)
-                if last:
-                    o_quant(i, b, b + 1)
-                    o_store(i, b, b + 1)
-            if not last:
-                res_store(i)
-                o_quant(i)
-                o_store(i)
-
-        for i in range(NT + 3):
-            if i == 0:
-                make_wr(0)
-            if i < NT:
-                make_q(i)
-            if i == 0:
-                make_wr(1)
-            if i == 0:
-                for j in range(4):
-                    x_turn(j)
-                    x_copy(j, "act")
-                w_copy(("wx",), wx_raw, "dve")
-                x_quant(0)
-                w_quant(("wx",))
-                w_copy(("wphi", 0), wphi_raw[0], "act")
-                x_quant(1)
-                w_copy(("wphi", 1), wphi_raw[1], "act")
-                w_quant(("wphi", 0))
-                w_quant(("wphi", 1))
-            k = i - 1
-            if 0 <= k < NT:
-                make_r(k)
-            k = i - 3
-            if 0 <= k < NT:
-                s2(k)
-                for a in range(A):
-                    phi(k, a)
-                make_out(k)
+        q_turn(1, 0)
+        q_turn(1, 1)
+        q_mul(1, 0)
+        wr_copy(3, 0, "act", 0, 52)
+        wr_copy(3, 0, "dve", 52, P)
+        q_mul(1, 1)
+        wr_copy(1, 1, "act", 0, 64)
+        w_quant(("wr", 3, 0))
+        wr_copy(1, 1, "dve", 64, P)
+        wr_copy(2, 0, "act", 0, 64)
+        wr_copy(2, 0, "dve", 64, P)
+        w_quant(("wr", 1, 1))
+        q_turn(0, 0)
+        w_quant(("wr", 2, 0))
+        q_turn(0, 1)
+        q_mul(0, 0)
+        wr_copy(1, 0, "act", 0, 128)
+        q_mul(0, 1)
+        q_quant(1)
+        q_turn(2, 0)
+        q_quant(0)
+        q_turn(2, 1)
+        q_mul(2, 0)
+        wr_copy(0, 0, "act", 0, 76)
+        wr_copy(0, 0, "dve", 76, P)
+        w_quant(("wr", 1, 0))
+        q_mul(2, 1)
+        wr_copy(2, 1, "act", 0, 128)
+        w_quant(("wr", 0, 0))
+        q_turn(3, 0)
+        q_quant(2)
+        s1(0, 0)
+        q_mul(3, 0)
+        wr_copy(0, 1, "dve", 52, P)
+        wr_copy(0, 1, "act", 0, 52)
+        q_turn(3, 1)
+        w_quant(("wr", 2, 1))
+        s1(1, 0)
+        wr_copy(3, 1, "act", 0, 96)
+        wr_copy(3, 1, "dve", 96, P)
+        w_quant(("wr", 0, 1))
+        r_mul(0, 0)
+        r_mul(1, 0)
+        s1(2, 0)
+        w_copy(("wphi", 1), wphi_raw[1], "act")
+        w_quant(("wr", 3, 1))
+        q_mul(3, 1)
+        s1(0, 1)
+        r_mul(2, 0)
+        q_quant(3)
+        s1(1, 1)
+        w_copy(("wphi", 0), wphi_raw[0], "act")
+        r_mul(0, 1)
+        w_quant(("wphi", 1))
+        q_turn(4, 0)
+        r_quant(0)
+        r_mul(1, 1)
+        q_turn(4, 1)
+        q_mul(4, 0)
+        x_turn(0)
+        w_copy(("wx",), wx_raw, "act")
+        q_mul(4, 1)
+        x_turn(1)
+        w_quant(("wphi", 0))
+        q_turn(5, 0)
+        r_quant(1)
+        q_turn(5, 1)
+        q_mul(5, 0)
+        s1(2, 1)
+        q_mul(5, 1)
+        x_copy(0, "act")
+        q_quant(4)
+        x_copy(1, "act")
+        q_turn(6, 0)
+        w_quant(("wx",))
+        q_turn(6, 1)
+        x_quant(0)
+        x_turn(2)
+        q_mul(6, 0)
+        s2(0)
+        q_mul(6, 1)
+        x_copy(2, "act")
+        r_mul(2, 1)
+        q_turn(7, 0)
+        phi(0, 0)
+        q_quant(5)
+        q_turn(7, 1)
+        phi(0, 1)
+        r_quant(2)
+        q_mul(7, 0)
+        s2(1)
+        phi(0, 2)
+        q_mul(7, 1)
+        phi(0, 3)
+        x_turn(3)
+        mix(0, 0)
+        phi(1, 0)
+        s1(3, 0)
+        mix(0, 1)
+        phi(1, 1)
+        mix(0, 2)
+        phi(1, 2)
+        mix(0, 3)
+        res_store(0)
+        s1(3, 1)
+        phi(1, 3)
+        r_mul(3, 0)
+        x_copy(3, "act")
+        q_quant(6)
+        o_cast(0, "act", 0, 256)
+        s2(2)
+        x_quant(1)
+        s1(4, 0)
+        q_quant(7)
+        o_cast(0, "act", 256, 512)
+        r_mul(3, 1)
+        mix(1, 0)
+        o_turn(0, 0, 1)
+        phi(2, 0)
+        s1(4, 1)
+        mix(1, 1)
+        phi(2, 1)
+        mix(1, 2)
+        phi(2, 2)
+        mix(1, 3)
+        res_store(1)
+        phi(2, 3)
+        o_turn(0, 1, 2)
+        r_quant(3)
+        o_copy(0, 0, "act")
+        r_mul(4, 0)
+        s2(3)
+        o_cast(1, "act", 256, 512)
+        r_mul(4, 1)
+        o_cast(1, "dve", 0, 256)
+        s1(5, 0)
+        o_copy(0, 1, "act")
+        mix(2, 0)
+        phi(3, 0)
+        mix(2, 1)
+        o_turn(1, 1, 2)
+        phi(3, 1)
+        mix(2, 2)
+        o_turn(1, 0, 1)
+        phi(3, 2)
+        s1(5, 1)
+        mix(2, 3)
+        res_store(2)
+        phi(3, 3)
+        r_quant(4)
+        o_cast(2, "act", 0, 256)
+        mix(3, 0)
+        s2(4)
+        mix(3, 1)
+        o_cast(2, "act", 256, 512)
+        mix(3, 2)
+        mix(3, 3)
+        res_store(3)
+        phi(4, 0)
+        r_mul(5, 0)
+        phi(4, 1)
+        o_quant(0)
+        o_store(0)
+        s1(6, 0)
+        phi(4, 2)
+        r_mul(5, 1)
+        phi(4, 3)
+        mix(4, 0)
+        s1(6, 1)
+        o_copy(1, 1, "act")
+        r_quant(5)
+        o_copy(1, 0, "act")
+        mix(4, 1)
+        o_turn(2, 0, 1)
+        o_cast(3, "act", 0, 256)
+        mix(4, 2)
+        o_turn(2, 1, 2)
+        mix(4, 3)
+        res_store(4)
+        s2(5)
+        o_cast(3, "act", 256, 512)
+        o_quant(1)
+        o_store(1)
+        r_mul(6, 0)
+        phi(5, 0)
+        r_mul(6, 1)
+        s1(7, 0)
+        phi(5, 1)
+        o_cast(4, "dve", 0, 256)
+        phi(5, 2)
+        r_quant(6)
+        s1(7, 1)
+        o_cast(4, "dve", 256, 512)
+        phi(5, 3)
+        mix(5, 0)
+        o_copy(2, 0, "act")
+        mix(5, 1)
+        s2(6)
+        o_copy(2, 1, "act")
+        mix(5, 2)
+        o_turn(3, 0, 1)
+        mix(5, 3)
+        res_store(5)
+        phi(6, 0)
+        o_turn(3, 1, 2)
+        phi(6, 1)
+        o_quant(2)
+        o_store(2)
+        phi(6, 2)
+        r_mul(7, 0)
+        phi(6, 3)
+        r_mul(7, 1)
+        o_copy(3, 0, "act")
+        o_cast(5, "dve", 0, 256)
+        o_copy(3, 1, "act")
+        o_turn(4, 0, 1)
+        r_quant(7)
+        mix(6, 0)
+        o_cast(5, "act", 256, 512)
+        s2(7)
+        o_quant(3)
+        o_store(3)
+        scale_store(0, 4)
+        o_turn(4, 1, 2)
+        mix(6, 1)
+        o_copy(4, 0, "act")
+        mix(6, 2)
+        phi(7, 0)
+        o_turn(5, 0, 1)
+        mix(6, 3)
+        res_store(6)
+        phi(7, 1)
+        o_cast(6, "dve", 0, 256)
+        phi(7, 2)
+        mix(7, 0)
+        phi(7, 3)
+        o_copy(4, 1, "act")
+        mix(7, 1)
+        res_store(7, 0, 2)
+        o_cast(6, "act", 256, 512)
+        mix(7, 2)
+        o_turn(5, 1, 2)
+        o_quant(4)
+        o_store(4)
+        o_copy(5, 0, "act")
+        mix(7, 3)
+        res_store(7, 2, 4)
+        o_copy(5, 1, "act")
+        o_turn(6, 0, 1)
+        o_cast(7, "dve", 0, 128)
+        o_cast(7, "dve", 128, 256)
+        o_turn(6, 1, 2)
+        o_copy(6, 0, "act")
+        o_cast(7, "dve", 256, 384)
+        o_cast(7, "dve", 384, 512)
+        o_copy(6, 1, "act")
+        o_quant(5)
+        o_store(5)
+        o_turn(7, 0, 1)
+        o_turn(7, 1, 2)
+        o_quant(6)
+        o_store(6)
+        o_copy(7, 0, "act")
+        o_copy(7, 1, "act")
+        o_quant(7, 0, 1)
+        o_store(7, 0, 1)
+        o_quant(7, 1, 2)
+        o_store(7, 1, 2)
+        scale_store(4, 8)

@@ -38,11 +38,15 @@ def tile_statisticalrecurrentunitmultiscale_x1_kernel(
 
         ctx.enter_context(tc.manual_schedule())
 
-        gmu_t = keep.tile([P, G1, 2, 2], BF16, name="gmu_t")
-        gr_t = keep.tile([P, G2, PACK], BF16, name="gr_t")
+        gate_rows = keep.tile([P, KP], BF16, name="gate_rows", align_bytes=64)
+        gates = keep.tile([P, G1 + G2, PACK], BF16, name="gates")
         mu_sb = [keep.tile([P, C], BF16, name=f"mu_{i}", align_bytes=64) for i in range(NT)]
         x_sb = keep.tile([P, NT, D], BF16, name="x_sb", align_bytes=64)
-        wr_raw = [work.tile([P, PACK, R], BF16, name=f"wr_raw_{g}", tag="big", bufs=4, align_bytes=64) for g in range(G1)]
+        wr_raw = {
+            (g, h): work.tile([P, PACK, KP], BF16, name=f"wr_raw_{g}_{h}", tag="big", bufs=8, align_bytes=64)
+            for g in range(G1)
+            for h in range(2)
+        }
         wx_raw = keep.tile([P, PACK, S], BF16, name="wx_raw", align_bytes=64)
         wphi_raw = [keep.tile([P, PACK, S], BF16, name=f"wphi_raw_{g}", align_bytes=64) for g in range(G2)]
 
@@ -51,9 +55,8 @@ def tile_statisticalrecurrentunitmultiscale_x1_kernel(
 
         def load_wr(g, h):
             src = wr[KP * g : KP * (g + 1), :].rearrange("(p j) c -> p j c", j=PACK)
-            nc.sync.dma_start(out=wr_raw[g][:, :, KP * h : KP * (h + 1)], in_=src[:, :, KP * h : KP * (h + 1)])
+            nc.sync.dma_start(out=wr_raw[g, h][:], in_=src[:, :, KP * h : KP * (h + 1)])
 
-        gates = nc.scalar
         def load_x():
             nc.sync.dma_start(out=x_sb[:], in_=x.rearrange("(i p) d -> p i d", p=P))
 
@@ -65,11 +68,16 @@ def tile_statisticalrecurrentunitmultiscale_x1_kernel(
                 out=wphi_raw[g][:], in_=wphi[KP * g : KP * (g + 1), :].rearrange("(p j) c -> p j c", j=PACK)
             )
 
-        gates.dma_start(out=gmu_t[:], in_=gmu.rearrange("(g p u e) -> p g u e", p=P, u=2, e=2))
-        gates.dma_start(out=gr_t[:], in_=gr.rearrange("(g p t) -> p g t", p=P, t=PACK))
+        nc.vector.memset(gate_rows[:], 0.0)
+
+        def load_gates():
+            nc.sync.dma_start(out=gate_rows[0:G1, :], in_=gmu.rearrange("(g c) -> g c", g=G1))
+            nc.sync.dma_start(out=gate_rows[G1 : G1 + G2, :], in_=gr.rearrange("(g c) -> g c", g=G2))
+
         load_mu(1)
-        load_wr(3, 0)
+        load_gates()
         load_wr(1, 1)
+        load_wr(3, 0)
         load_wr(2, 0)
         load_mu(0)
         load_wr(1, 0)
@@ -80,9 +88,9 @@ def tile_statisticalrecurrentunitmultiscale_x1_kernel(
         load_wr(0, 1)
         load_wr(3, 1)
         load_wphi(1)
+        load_mu(4)
         load_wphi(0)
         load_x()
-        load_mu(4)
         load_wx()
         load_mu(5)
         load_mu(7)
@@ -94,6 +102,14 @@ def tile_statisticalrecurrentunitmultiscale_x1_kernel(
         nc.vector.memset(warm[:], 0.0)
         nc.scalar.activation(out=warm[:], in_=warm[:], func=ACTF.Relu)
 
+        gate_ps = psum.tile([P, 2, P], F32, name="gate_ps", tag="y_ps", bufs=2)
+        for u in range(2):
+            nc.tensor.transpose(gate_ps[:, u, :], gate_rows[:].bitcast(F32)[:, u : KP // 2 : 2], ident[:])
+        nc.scalar.copy(
+            out=gates[:].rearrange("p g t -> p (g t)").bitcast(F32).rearrange("p (g u) -> p g u", u=2),
+            in_=gate_ps[:, :, 0 : G1 + G2].rearrange("p u g -> p g u"),
+        )
+
         codes, scales, grouped = {}, {}, {}
 
         def copy_on(engine, out, in_):
@@ -102,12 +118,12 @@ def tile_statisticalrecurrentunitmultiscale_x1_kernel(
             else:
                 nc.vector.tensor_copy(out=out, in_=in_)
 
-        def wr_copy(g, h, engine, m0, m1):
+        def wr_copy(g, h, engine, t0, t1):
             if ("wr", g, h) not in grouped:
                 grouped["wr", g, h] = work.tile([P, PACK, P, PACK], BF16, name="w_grouped", tag="w_grouped", bufs=4, align_bytes=64)
-            raw = wr_raw[g][:, :, KP * h : KP * (h + 1)].rearrange("p j (m t) -> p m t j", t=PACK)
+            raw = wr_raw[g, h][:].rearrange("p j (m t) -> p m t j", t=PACK)
             copy_on(
-                engine, grouped["wr", g, h][:, :, m0:m1].rearrange("p t m j -> p m t j"), raw[:, m0:m1]
+                engine, grouped["wr", g, h][:, t0:t1].rearrange("p t m j -> p m t j"), raw[:, :, t0:t1]
             )
 
         def w_copy(key, raw, engine):
@@ -142,7 +158,7 @@ def tile_statisticalrecurrentunitmultiscale_x1_kernel(
             nc.vector.tensor_tensor(
                 out=q_gr[i][:, 2 * b : 2 * b + 2],
                 in0=src.rearrange("p u (g r e) -> p g r u e", g=2, e=2),
-                in1=gmu_t[:, 2 * b : 2 * b + 2].unsqueeze(2).to_broadcast([P, 2, P, 2, 2]),
+                in1=gates[:, 2 * b : 2 * b + 2].rearrange("p g (u e) -> p g u e", e=2).unsqueeze(2).to_broadcast([P, 2, P, 2, 2]),
                 op=ALU.mult,
             )
 
@@ -209,7 +225,7 @@ def tile_statisticalrecurrentunitmultiscale_x1_kernel(
                 out=r_gr[i][:, h],
                 in0=z_ps[i, h][:].rearrange("p t n -> p n t"),
                 scalar=0.0,
-                in1=gr_t[:, h, :].unsqueeze(1).to_broadcast([P, P, PACK]),
+                in1=gates[:, G1 + h, :].unsqueeze(1).to_broadcast([P, P, PACK]),
                 op0=ALU.max,
                 op1=ALU.mult,
             )
@@ -256,42 +272,40 @@ def tile_statisticalrecurrentunitmultiscale_x1_kernel(
             nc.scalar.activation(out=pt[:], in_=y_ps[i][:], func=ACTF.Relu, scale=1.0 - ALPHA[a])
 
         def mix(i, a):
-            if i not in res:
-                res[i] = work.tile([P, C], F32, name="res", tag="big", bufs=4, align_bytes=64)
-            cols = slice(S * a, S * (a + 1))
+            b, k = a // 2, a % 2
+            if (i, b) not in res:
+                res[i, b] = work.tile([P, C // 2], F32, name="res", tag="big", bufs=8, align_bytes=64)
             nc.vector.scalar_tensor_tensor(
-                out=res[i][:, cols],
-                in0=mu_sb[i][:, cols],
+                out=res[i, b][:, S * k : S * (k + 1)],
+                in0=mu_sb[i][:, S * a : S * (a + 1)],
                 scalar=ALPHA[a],
                 in1=part[i, a][:],
                 op0=ALU.mult,
                 op1=ALU.add,
             )
 
-        def res_store(i, a0=0, a1=A):
-            cols = slice(S * a0, S * a1)
-            nc.sync.dma_start(out=out_0[P * i : P * (i + 1), cols], in_=res[i][:, cols])
+        def res_store(i, b):
+            w = C // 2
+            nc.sync.dma_start(out=out_0[P * i : P * (i + 1), w * b : w * (b + 1)], in_=res[i, b][:])
 
         o_bf, o_ps, o_gr, o_codes, o_scales = {}, {}, {}, {}, {}
 
-        def o_cast(i, engine, w0, w1):
-            if i not in o_bf:
-                o_bf[i] = work.tile([P, 2, C // 4, 2], BF16, name="o_bf", tag="o_bf", bufs=2, align_bytes=64)
+        def o_cast(i, b, engine, w0=0, w1=C // 8):
+            if (i, b) not in o_bf:
+                o_bf[i, b] = work.tile([P, 2, C // 8, 2], BF16, name="o_bf", tag="o_bf", bufs=4, align_bytes=64)
             copy_on(
                 engine,
-                o_bf[i][:, :, w0:w1],
-                res[i][:, 4 * w0 : 4 * w1].rearrange("p (w u e) -> p u w e", u=2, e=2),
+                o_bf[i, b][:, :, w0:w1],
+                res[i, b][:, 4 * w0 : 4 * w1].rearrange("p (w u e) -> p u w e", u=2, e=2),
             )
 
-        def o_turn(i, b0=0, b1=2):
-            for b in range(b0, b1):
-                ps = psum.tile([P, 2, 2, P], F32, name="o_ps", tag="o_ps", bufs=2)
-                o_ps[i, b] = ps
-                for u in range(2):
-                    words = o_bf[i][:, u].rearrange("p w e -> p (w e)").bitcast(F32)
-                    for k in range(2):
-                        g = 2 * b + k
-                        nc.tensor.transpose(ps[:, u, k, :], words[:, P * g : P * (g + 1)], ident[:])
+        def o_turn(i, b):
+            ps = psum.tile([P, 2, 2, P], F32, name="o_ps", tag="o_ps", bufs=2)
+            o_ps[i, b] = ps
+            for u in range(2):
+                words = o_bf[i, b][:, u].rearrange("p w e -> p (w e)").bitcast(F32)
+                for k in range(2):
+                    nc.tensor.transpose(ps[:, u, k, :], words[:, P * k : P * (k + 1)], ident[:])
 
         def o_copy(i, b, engine="act"):
             if i not in o_gr:
@@ -302,7 +316,7 @@ def tile_statisticalrecurrentunitmultiscale_x1_kernel(
                 o_ps[i, b][:].rearrange("p u k r -> p (k r) u"),
             )
 
-        scales_all = keep.tile([P, G1, N], U8, name="o_scales", align_bytes=64)
+        scales_half = [keep.tile([P, G1, N // 2], U8, name=f"o_scales_{k}", align_bytes=64) for k in range(2)]
 
         def o_quant(i, b0=0, b1=2):
             if i not in o_codes:
@@ -310,7 +324,7 @@ def tile_statisticalrecurrentunitmultiscale_x1_kernel(
             for g in range(2 * b0, 2 * b1):
                 nc.vector.quantize_mx(
                     out=o_codes[i][:, g, :].bitcast(FP8X4),
-                    scales=scales_all[:, g, P * i : P * (i + 1)],
+                    scales=scales_half[i // 4][:, g, P * (i % 4) : P * (i % 4 + 1)],
                     in_=o_gr[i][:, g].rearrange("p n t -> p (n t)"),
                 )
 
@@ -321,89 +335,91 @@ def tile_statisticalrecurrentunitmultiscale_x1_kernel(
                 out=words[:, gs, KP * i : KP * (i + 1)].bitcast(I32), in_=o_codes[i][:, gs].bitcast(I32)
             )
 
-        def scale_store(i0, i1):
+        def scale_store(k):
+            w = N // 2
             rows = out_2.rearrange("g (q r) m -> q r g m", r=4)
             for q in range(4):
                 nc.sync.dma_start(
-                    out=rows[q, :, :, P * i0 : P * i1].bitcast(I32),
-                    in_=scales_all[32 * q : 32 * q + 4, :, P * i0 : P * i1].bitcast(I32),
+                    out=rows[q, :, :, w * k : w * (k + 1)].bitcast(I32),
+                    in_=scales_half[k][32 * q : 32 * q + 4].bitcast(I32),
                 )
 
         q_turn(1, 0)
         q_turn(1, 1)
         q_mul(1, 0)
-        wr_copy(3, 0, "act", 0, 52)
-        wr_copy(3, 0, "dve", 52, P)
+        wr_copy(1, 1, "act", 0, 2)
+        wr_copy(1, 1, "dve", 2, PACK)
         q_mul(1, 1)
-        wr_copy(1, 1, "act", 0, 64)
-        w_quant(("wr", 3, 0))
-        wr_copy(1, 1, "dve", 64, P)
-        wr_copy(2, 0, "act", 0, 64)
-        wr_copy(2, 0, "dve", 64, P)
+        wr_copy(3, 0, "act", 0, 2)
+        wr_copy(3, 0, "dve", 2, PACK)
         w_quant(("wr", 1, 1))
+        wr_copy(2, 0, "act", 0, 2)
+        wr_copy(2, 0, "dve", 2, PACK)
+        w_quant(("wr", 3, 0))
         q_turn(0, 0)
         w_quant(("wr", 2, 0))
         q_turn(0, 1)
         q_mul(0, 0)
-        wr_copy(1, 0, "act", 0, 128)
+        wr_copy(1, 0, "act", 0, 3)
+        wr_copy(1, 0, "dve", 3, PACK)
         q_mul(0, 1)
-        q_quant(1)
         q_turn(2, 0)
-        q_quant(0)
+        q_quant(1)
         q_turn(2, 1)
-        q_mul(2, 0)
-        wr_copy(0, 0, "act", 0, 76)
-        wr_copy(0, 0, "dve", 76, P)
+        q_quant(0)
         w_quant(("wr", 1, 0))
-        q_mul(2, 1)
-        wr_copy(2, 1, "act", 0, 128)
+        wr_copy(0, 0, "act", 0, 2)
+        wr_copy(0, 0, "dve", 2, PACK)
+        q_mul(2, 0)
+        wr_copy(2, 1, "act", 0, 4)
         w_quant(("wr", 0, 0))
+        q_mul(2, 1)
         q_turn(3, 0)
-        q_quant(2)
         s1(0, 0)
-        q_mul(3, 0)
-        wr_copy(0, 1, "dve", 52, P)
-        wr_copy(0, 1, "act", 0, 52)
-        q_turn(3, 1)
-        w_quant(("wr", 2, 1))
+        q_quant(2)
+        wr_copy(0, 1, "dve", 2, PACK)
+        wr_copy(0, 1, "act", 0, 2)
         s1(1, 0)
-        wr_copy(3, 1, "act", 0, 96)
-        wr_copy(3, 1, "dve", 96, P)
-        w_quant(("wr", 0, 1))
+        w_quant(("wr", 2, 1))
         r_mul(0, 0)
-        r_mul(1, 0)
+        wr_copy(3, 1, "act", 0, 3)
+        q_turn(3, 1)
+        wr_copy(3, 1, "dve", 3, PACK)
+        w_quant(("wr", 0, 1))
         s1(2, 0)
+        r_mul(1, 0)
         w_copy(("wphi", 1), wphi_raw[1], "act")
+        q_mul(3, 0)
         w_quant(("wr", 3, 1))
+        q_turn(4, 0)
         q_mul(3, 1)
         s1(0, 1)
-        r_mul(2, 0)
-        q_quant(3)
-        s1(1, 1)
-        w_copy(("wphi", 0), wphi_raw[0], "act")
-        r_mul(0, 1)
-        w_quant(("wphi", 1))
-        q_turn(4, 0)
-        r_quant(0)
-        r_mul(1, 1)
-        q_turn(4, 1)
         q_mul(4, 0)
-        x_turn(0)
-        w_copy(("wx",), wx_raw, "act")
+        r_mul(2, 0)
+        w_copy(("wphi", 0), wphi_raw[0], "act")
+        q_turn(4, 1)
+        w_quant(("wphi", 1))
+        s1(1, 1)
+        r_mul(0, 1)
         q_mul(4, 1)
+        r_quant(0)
+        x_turn(0)
+        q_quant(3)
+        w_copy(("wx",), wx_raw, "act")
         x_turn(1)
         w_quant(("wphi", 0))
         q_turn(5, 0)
-        r_quant(1)
+        r_mul(1, 1)
         q_turn(5, 1)
-        q_mul(5, 0)
-        s1(2, 1)
-        q_mul(5, 1)
-        x_copy(0, "act")
         q_quant(4)
-        x_copy(1, "act")
-        q_turn(6, 0)
+        s1(2, 1)
+        q_mul(5, 0)
+        x_copy(0, "act")
         w_quant(("wx",))
+        x_copy(1, "act")
+        q_mul(5, 1)
+        q_turn(6, 0)
+        r_quant(1)
         q_turn(6, 1)
         x_quant(0)
         x_turn(2)
@@ -417,178 +433,185 @@ def tile_statisticalrecurrentunitmultiscale_x1_kernel(
         q_quant(5)
         q_turn(7, 1)
         phi(0, 1)
-        r_quant(2)
-        q_mul(7, 0)
+        q_quant(6)
         s2(1)
         phi(0, 2)
-        q_mul(7, 1)
+        q_mul(7, 0)
         phi(0, 3)
         x_turn(3)
-        mix(0, 0)
+        q_mul(7, 1)
         phi(1, 0)
+        mix(0, 0)
         s1(3, 0)
-        mix(0, 1)
         phi(1, 1)
-        mix(0, 2)
+        mix(0, 1)
+        res_store(0, 0)
         phi(1, 2)
-        mix(0, 3)
-        res_store(0)
+        mix(0, 2)
         s1(3, 1)
         phi(1, 3)
-        r_mul(3, 0)
+        mix(0, 3)
+        res_store(0, 1)
         x_copy(3, "act")
-        q_quant(6)
-        o_cast(0, "act", 0, 256)
-        s2(2)
-        x_quant(1)
-        s1(4, 0)
         q_quant(7)
-        o_cast(0, "act", 256, 512)
-        r_mul(3, 1)
+        o_cast(0, 0, "act")
+        x_quant(1)
+        r_quant(2)
+        o_cast(0, 1, "act")
         mix(1, 0)
-        o_turn(0, 0, 1)
-        phi(2, 0)
-        s1(4, 1)
+        o_turn(0, 0)
         mix(1, 1)
-        phi(2, 1)
-        mix(1, 2)
-        phi(2, 2)
-        mix(1, 3)
-        res_store(1)
-        phi(2, 3)
-        o_turn(0, 1, 2)
-        r_quant(3)
+        res_store(1, 0)
+        s2(2)
         o_copy(0, 0, "act")
-        r_mul(4, 0)
-        s2(3)
-        o_cast(1, "act", 256, 512)
-        r_mul(4, 1)
-        o_cast(1, "dve", 0, 256)
-        s1(5, 0)
-        o_copy(0, 1, "act")
+        mix(1, 2)
+        o_turn(0, 1)
+        mix(1, 3)
+        res_store(1, 1)
+        phi(2, 0)
+        r_mul(3, 0)
+        phi(2, 1)
+        r_mul(3, 1)
+        s1(4, 0)
+        phi(2, 2)
+        o_cast(1, 0, "dve")
+        phi(2, 3)
+        r_quant(3)
+        o_cast(1, 1, "act")
         mix(2, 0)
-        phi(3, 0)
+        s1(4, 1)
         mix(2, 1)
-        o_turn(1, 1, 2)
-        phi(3, 1)
+        res_store(2, 0)
+        o_copy(0, 1, "act")
         mix(2, 2)
-        o_turn(1, 0, 1)
-        phi(3, 2)
-        s1(5, 1)
+        s2(3)
+        o_cast(2, 0, "act")
         mix(2, 3)
-        res_store(2)
-        phi(3, 3)
-        r_quant(4)
-        o_cast(2, "act", 0, 256)
-        mix(3, 0)
-        s2(4)
-        mix(3, 1)
-        o_cast(2, "act", 256, 512)
-        mix(3, 2)
-        mix(3, 3)
-        res_store(3)
-        phi(4, 0)
-        r_mul(5, 0)
-        phi(4, 1)
+        res_store(2, 1)
+        o_turn(1, 0)
+        r_mul(4, 0)
+        o_turn(1, 1)
+        phi(3, 0)
+        r_mul(4, 1)
+        s1(5, 0)
+        phi(3, 1)
         o_quant(0)
         o_store(0)
-        s1(6, 0)
-        phi(4, 2)
-        r_mul(5, 1)
-        phi(4, 3)
-        mix(4, 0)
-        s1(6, 1)
-        o_copy(1, 1, "act")
-        r_quant(5)
+        phi(3, 2)
+        r_quant(4)
+        phi(3, 3)
+        s1(5, 1)
+        mix(3, 0)
+        o_cast(2, 1, "act")
+        r_mul(5, 0)
+        mix(3, 1)
+        res_store(3, 0)
+        s2(4)
         o_copy(1, 0, "act")
-        mix(4, 1)
-        o_turn(2, 0, 1)
-        o_cast(3, "act", 0, 256)
-        mix(4, 2)
-        o_turn(2, 1, 2)
-        mix(4, 3)
-        res_store(4)
-        s2(5)
-        o_cast(3, "act", 256, 512)
+        mix(3, 2)
+        s1(6, 0)
+        o_copy(1, 1, "act")
+        mix(3, 3)
+        res_store(3, 1)
+        phi(4, 0)
+        r_mul(5, 1)
+        phi(4, 1)
+        o_turn(2, 0)
         o_quant(1)
         o_store(1)
+        o_turn(2, 1)
+        phi(4, 2)
+        s1(6, 1)
+        r_quant(5)
         r_mul(6, 0)
+        phi(4, 3)
+        mix(4, 0)
+        o_cast(3, 0, "act")
+        s2(5)
+        mix(4, 1)
+        res_store(4, 0)
+        o_cast(3, 1, "act")
+        mix(4, 2)
+        s1(7, 0)
+        mix(4, 3)
+        res_store(4, 1)
         phi(5, 0)
         r_mul(6, 1)
-        s1(7, 0)
         phi(5, 1)
-        o_cast(4, "dve", 0, 256)
+        o_cast(4, 0, "dve")
+        s1(7, 1)
         phi(5, 2)
         r_quant(6)
-        s1(7, 1)
-        o_cast(4, "dve", 256, 512)
+        o_cast(4, 1, "dve")
         phi(5, 3)
-        mix(5, 0)
-        o_copy(2, 0, "act")
-        mix(5, 1)
         s2(6)
+        r_mul(7, 0)
+        o_copy(2, 0, "act")
+        mix(5, 0)
         o_copy(2, 1, "act")
-        mix(5, 2)
-        o_turn(3, 0, 1)
-        mix(5, 3)
-        res_store(5)
+        o_turn(3, 0)
+        mix(5, 1)
+        res_store(5, 0)
         phi(6, 0)
-        o_turn(3, 1, 2)
-        phi(6, 1)
+        o_turn(3, 1)
         o_quant(2)
         o_store(2)
+        phi(6, 1)
+        mix(5, 2)
         phi(6, 2)
-        r_mul(7, 0)
+        mix(5, 3)
+        res_store(5, 1)
         phi(6, 3)
         r_mul(7, 1)
         o_copy(3, 0, "act")
-        o_cast(5, "dve", 0, 256)
+        o_cast(5, 0, "dve")
         o_copy(3, 1, "act")
-        o_turn(4, 0, 1)
+        o_turn(4, 0)
         r_quant(7)
-        mix(6, 0)
-        o_cast(5, "act", 256, 512)
-        s2(7)
+        o_cast(5, 1, "act")
+        o_turn(4, 1)
         o_quant(3)
         o_store(3)
-        scale_store(0, 4)
-        o_turn(4, 1, 2)
-        mix(6, 1)
+        scale_store(0)
+        s2(7)
+        mix(6, 0)
         o_copy(4, 0, "act")
+        mix(6, 1)
+        res_store(6, 0)
+        o_copy(4, 1, "act")
+        o_turn(5, 0)
         mix(6, 2)
         phi(7, 0)
-        o_turn(5, 0, 1)
+        o_turn(5, 1)
         mix(6, 3)
-        res_store(6)
+        res_store(6, 1)
         phi(7, 1)
-        o_cast(6, "dve", 0, 256)
-        phi(7, 2)
-        mix(7, 0)
-        phi(7, 3)
-        o_copy(4, 1, "act")
-        mix(7, 1)
-        res_store(7, 0, 2)
-        o_cast(6, "act", 256, 512)
-        mix(7, 2)
-        o_turn(5, 1, 2)
         o_quant(4)
         o_store(4)
+        phi(7, 2)
+        o_cast(6, 0, "dve")
+        phi(7, 3)
+        mix(7, 0)
+        o_cast(6, 1, "act")
+        mix(7, 1)
+        res_store(7, 0)
+        mix(7, 2)
         o_copy(5, 0, "act")
         mix(7, 3)
-        res_store(7, 2, 4)
+        res_store(7, 1)
         o_copy(5, 1, "act")
-        o_turn(6, 0, 1)
-        o_cast(7, "dve", 0, 128)
-        o_cast(7, "dve", 128, 256)
-        o_turn(6, 1, 2)
+        o_turn(6, 0)
+        o_cast(7, 0, "dve", 0, 128)
+        o_turn(6, 1)
         o_copy(6, 0, "act")
-        o_cast(7, "dve", 256, 384)
-        o_cast(7, "dve", 384, 512)
+        o_cast(7, 0, "dve", 128, 256)
+        o_cast(7, 1, "dve", 0, 128)
         o_copy(6, 1, "act")
+        o_turn(7, 0)
+        o_cast(7, 1, "dve", 128, 256)
         o_quant(5)
         o_store(5)
-        o_turn(7, 0, 1)
-        o_turn(7, 1, 2)
+        o_turn(7, 1)
         o_quant(6)
         o_store(6)
         o_copy(7, 0, "act")
@@ -597,4 +620,4 @@ def tile_statisticalrecurrentunitmultiscale_x1_kernel(
         o_store(7, 0, 1)
         o_quant(7, 1, 2)
         o_store(7, 1, 2)
-        scale_store(4, 8)
+        scale_store(1)

@@ -39,7 +39,10 @@ def tile_statisticalrecurrentunitmultiscale_x1_kernel(
         ctx.enter_context(tc.manual_schedule())
 
         gate_rows = keep.tile([P, KP], BF16, name="gate_rows", align_bytes=64)
-        gates = keep.tile([P, G1 + G2, PACK], BF16, name="gates")
+        gate_perm = keep.tile([P, PACK, P], BF16, name="gate_perm", align_bytes=64)
+        gmu_t = keep.tile([P, G1, PACK], BF16, name="gmu_t")
+        gr_t = keep.tile([P, G2, PACK], BF16, name="gr_t")
+        ident_bf = keep.tile([P, P], BF16, name="ident_bf")
         mu_sb = [keep.tile([P, C], BF16, name=f"mu_{i}", align_bytes=64) for i in range(NT)]
         x_sb = keep.tile([P, NT, D], BF16, name="x_sb", align_bytes=64)
         wr_raw = {
@@ -64,9 +67,9 @@ def tile_statisticalrecurrentunitmultiscale_x1_kernel(
             nc.sync.dma_start(out=wx_raw[:], in_=wx.rearrange("(p j) c -> p j c", j=PACK))
 
         def load_wphi(g):
-            nc.sync.dma_start(
-                out=wphi_raw[g][:], in_=wphi[KP * g : KP * (g + 1), :].rearrange("(p j) c -> p j c", j=PACK)
-            )
+            src = wphi[KP * g : KP * (g + 1), :].rearrange("(s t v) c -> v s t c", t=PACK, v=2)
+            for v in range(2):
+                nc.sync.dma_start(out=wphi_raw[g][v:P:2, :, :], in_=src[v])
 
         nc.vector.memset(gate_rows[:], 0.0)
 
@@ -74,26 +77,26 @@ def tile_statisticalrecurrentunitmultiscale_x1_kernel(
             nc.sync.dma_start(out=gate_rows[0:G1, :], in_=gmu.rearrange("(g c) -> g c", g=G1))
             nc.sync.dma_start(out=gate_rows[G1 : G1 + G2, :], in_=gr.rearrange("(g c) -> g c", g=G2))
 
-        load_mu(1)
+        load_wr(3, 0)
         load_gates()
         load_wr(1, 1)
-        load_wr(3, 0)
-        load_wr(2, 0)
-        load_mu(0)
         load_wr(1, 0)
+        load_mu(1)
+        load_wr(2, 0)
         load_mu(2)
         load_wr(0, 0)
-        load_wr(2, 1)
-        load_mu(3)
-        load_wr(0, 1)
-        load_wr(3, 1)
+        load_mu(0)
         load_wphi(1)
+        load_wr(0, 1)
+        load_wr(2, 1)
         load_mu(4)
-        load_wphi(0)
+        load_wr(3, 1)
         load_x()
-        load_wx()
         load_mu(5)
+        load_wphi(0)
+        load_wx()
         load_mu(7)
+        load_mu(3)
         load_mu(6)
 
         ident = keep.tile([P, P], F32, name="ident")
@@ -106,9 +109,21 @@ def tile_statisticalrecurrentunitmultiscale_x1_kernel(
         for u in range(2):
             nc.tensor.transpose(gate_ps[:, u, :], gate_rows[:].bitcast(F32)[:, u : KP // 2 : 2], ident[:])
         nc.scalar.copy(
-            out=gates[:].rearrange("p g t -> p (g t)").bitcast(F32).rearrange("p (g u) -> p g u", u=2),
-            in_=gate_ps[:, :, 0 : G1 + G2].rearrange("p u g -> p g u"),
+            out=gmu_t[:].rearrange("p g t -> p (g t)").bitcast(F32).rearrange("p (g u) -> p g u", u=2),
+            in_=gate_ps[:, :, 0:G1].rearrange("p u g -> p g u"),
         )
+        make_identity(nc, ident_bf[:])
+        nc.gpsimd.tensor_copy(
+            out=gate_perm[:].rearrange("p t (s v) -> p t s v", v=2),
+            in_=gate_rows[:].rearrange("p (s t v) -> p t s v", t=PACK, v=2),
+        )
+
+        def gr_turn():
+            ps = psum.tile([P, PACK, P], BF16, name="gr_ps", tag="y_ps", bufs=2)
+            for t in range(PACK):
+                nc.tensor.transpose(ps[:, t, :], gate_perm[:, t, :], ident_bf[:])
+            nc.scalar.copy(out=gr_t[:], in_=ps[:, :, G1 : G1 + G2].rearrange("p t g -> p g t"))
+
 
         codes, scales, grouped = {}, {}, {}
 
@@ -118,12 +133,13 @@ def tile_statisticalrecurrentunitmultiscale_x1_kernel(
             else:
                 nc.vector.tensor_copy(out=out, in_=in_)
 
-        def wr_copy(g, h, engine, t0, t1):
-            if ("wr", g, h) not in grouped:
-                grouped["wr", g, h] = work.tile([P, PACK, P, PACK], BF16, name="w_grouped", tag="w_grouped", bufs=4, align_bytes=64)
-            raw = wr_raw[g, h][:].rearrange("p j (m t) -> p m t j", t=PACK)
+        def wr_copy(g, h, engine):
+            gt = work.tile([P, PACK, P, PACK], BF16, name="w_grouped", tag="w_grouped", bufs=4, align_bytes=64)
+            grouped["wr", g, h] = gt
             copy_on(
-                engine, grouped["wr", g, h][:, t0:t1].rearrange("p t m j -> p m t j"), raw[:, :, t0:t1]
+                engine,
+                gt[:].rearrange("p t (s v) j -> p s t v j", v=2),
+                wr_raw[g, h][:].rearrange("p j (s t v) -> p s t v j", t=PACK, v=2),
             )
 
         def w_copy(key, raw, engine):
@@ -158,7 +174,7 @@ def tile_statisticalrecurrentunitmultiscale_x1_kernel(
             nc.vector.tensor_tensor(
                 out=q_gr[i][:, 2 * b : 2 * b + 2],
                 in0=src.rearrange("p u (g r e) -> p g r u e", g=2, e=2),
-                in1=gates[:, 2 * b : 2 * b + 2].rearrange("p g (u e) -> p g u e", e=2).unsqueeze(2).to_broadcast([P, 2, P, 2, 2]),
+                in1=gmu_t[:, 2 * b : 2 * b + 2].rearrange("p g (u e) -> p g u e", e=2).unsqueeze(2).to_broadcast([P, 2, P, 2, 2]),
                 op=ALU.mult,
             )
 
@@ -225,7 +241,7 @@ def tile_statisticalrecurrentunitmultiscale_x1_kernel(
                 out=r_gr[i][:, h],
                 in0=z_ps[i, h][:].rearrange("p t n -> p n t"),
                 scalar=0.0,
-                in1=gates[:, G1 + h, :].unsqueeze(1).to_broadcast([P, P, PACK]),
+                in1=gr_t[:, h, :].unsqueeze(1).to_broadcast([P, P, PACK]),
                 op0=ALU.max,
                 op1=ALU.mult,
             )
@@ -290,22 +306,19 @@ def tile_statisticalrecurrentunitmultiscale_x1_kernel(
 
         o_bf, o_ps, o_gr, o_codes, o_scales = {}, {}, {}, {}, {}
 
-        def o_cast(i, b, engine, w0=0, w1=C // 8):
+        def o_cast(i, b, engine, k0=0, k1=2):
             if (i, b) not in o_bf:
-                o_bf[i, b] = work.tile([P, 2, C // 8, 2], BF16, name="o_bf", tag="o_bf", bufs=4, align_bytes=64)
-            copy_on(
-                engine,
-                o_bf[i, b][:, :, w0:w1],
-                res[i, b][:, 4 * w0 : 4 * w1].rearrange("p (w u e) -> p u w e", u=2, e=2),
-            )
+                o_bf[i, b] = work.tile([P, C // 2], BF16, name="o_bf", tag="o_bf", bufs=4, align_bytes=64)
+            cols = slice(S * k0, S * k1)
+            copy_on(engine, o_bf[i, b][:, cols], res[i, b][:, cols])
 
         def o_turn(i, b):
             ps = psum.tile([P, 2, 2, P], F32, name="o_ps", tag="o_ps", bufs=2)
             o_ps[i, b] = ps
-            for u in range(2):
-                words = o_bf[i, b][:, u].rearrange("p w e -> p (w e)").bitcast(F32)
-                for k in range(2):
-                    nc.tensor.transpose(ps[:, u, k, :], words[:, P * k : P * (k + 1)], ident[:])
+            words = o_bf[i, b][:].bitcast(F32)
+            for k in range(2):
+                for u in range(2):
+                    nc.tensor.transpose(ps[:, u, k, :], words[:, 256 * k + u : 256 * (k + 1) : 2], ident[:])
 
         def o_copy(i, b, engine="act"):
             if i not in o_gr:
@@ -344,280 +357,274 @@ def tile_statisticalrecurrentunitmultiscale_x1_kernel(
                     in_=scales_half[k][32 * q : 32 * q + 4].bitcast(I32),
                 )
 
+        wr_copy(3, 0, "dve")
+        wr_copy(1, 1, "act")
+        w_quant(("wr", 3, 0))
+        wr_copy(1, 0, "dve")
         q_turn(1, 0)
+        w_quant(("wr", 1, 1))
         q_turn(1, 1)
         q_mul(1, 0)
-        wr_copy(1, 1, "act", 0, 2)
-        wr_copy(1, 1, "dve", 2, PACK)
+        wr_copy(2, 0, "act")
+        w_quant(("wr", 1, 0))
         q_mul(1, 1)
-        wr_copy(3, 0, "act", 0, 2)
-        wr_copy(3, 0, "dve", 2, PACK)
-        w_quant(("wr", 1, 1))
-        wr_copy(2, 0, "act", 0, 2)
-        wr_copy(2, 0, "dve", 2, PACK)
-        w_quant(("wr", 3, 0))
-        q_turn(0, 0)
-        w_quant(("wr", 2, 0))
-        q_turn(0, 1)
-        q_mul(0, 0)
-        wr_copy(1, 0, "act", 0, 3)
-        wr_copy(1, 0, "dve", 3, PACK)
-        q_mul(0, 1)
         q_turn(2, 0)
         q_quant(1)
         q_turn(2, 1)
-        q_quant(0)
-        w_quant(("wr", 1, 0))
-        wr_copy(0, 0, "act", 0, 2)
-        wr_copy(0, 0, "dve", 2, PACK)
         q_mul(2, 0)
-        wr_copy(2, 1, "act", 0, 4)
-        w_quant(("wr", 0, 0))
+        wr_copy(0, 0, "act")
         q_mul(2, 1)
-        q_turn(3, 0)
-        s1(0, 0)
+        w_quant(("wr", 2, 0))
+        q_turn(0, 0)
         q_quant(2)
-        wr_copy(0, 1, "dve", 2, PACK)
-        wr_copy(0, 1, "act", 0, 2)
-        s1(1, 0)
-        w_quant(("wr", 2, 1))
-        r_mul(0, 0)
-        wr_copy(3, 1, "act", 0, 3)
-        q_turn(3, 1)
-        wr_copy(3, 1, "dve", 3, PACK)
-        w_quant(("wr", 0, 1))
-        s1(2, 0)
-        r_mul(1, 0)
+        q_turn(0, 1)
+        q_mul(0, 0)
+        q_mul(0, 1)
         w_copy(("wphi", 1), wphi_raw[1], "act")
-        q_mul(3, 0)
-        w_quant(("wr", 3, 1))
-        q_turn(4, 0)
-        q_mul(3, 1)
-        s1(0, 1)
-        q_mul(4, 0)
-        r_mul(2, 0)
-        w_copy(("wphi", 0), wphi_raw[0], "act")
-        q_turn(4, 1)
+        w_quant(("wr", 0, 0))
+        wr_copy(0, 1, "dve")
+        s1(1, 0)
+        q_quant(0)
+        wr_copy(2, 1, "act")
+        s1(2, 0)
+        w_quant(("wr", 0, 1))
         w_quant(("wphi", 1))
+        q_turn(4, 0)
+        gr_turn()
+        r_mul(1, 0)
+        q_turn(4, 1)
+        r_mul(2, 0)
+        wr_copy(3, 1, "act")
+        s1(0, 0)
+        w_quant(("wr", 2, 1))
+        q_mul(4, 0)
+        q_mul(4, 1)
+        x_turn(0)
+        r_mul(0, 0)
+        x_turn(1)
+        q_quant(4)
+        x_copy(0, "act")
+        q_turn(5, 0)
+        w_quant(("wr", 3, 1))
+        x_copy(1, "act")
+        q_turn(5, 1)
+        q_mul(5, 0)
+        w_copy(("wphi", 0), wphi_raw[0], "act")
+        s1(0, 1)
+        x_quant(0)
+        q_mul(5, 1)
         s1(1, 1)
         r_mul(0, 1)
-        q_mul(4, 1)
-        r_quant(0)
-        x_turn(0)
-        q_quant(3)
-        w_copy(("wx",), wx_raw, "act")
-        x_turn(1)
-        w_quant(("wphi", 0))
-        q_turn(5, 0)
-        r_mul(1, 1)
-        q_turn(5, 1)
-        q_quant(4)
-        s1(2, 1)
-        q_mul(5, 0)
-        x_copy(0, "act")
-        w_quant(("wx",))
-        x_copy(1, "act")
-        q_mul(5, 1)
-        q_turn(6, 0)
-        r_quant(1)
-        q_turn(6, 1)
-        x_quant(0)
-        x_turn(2)
-        q_mul(6, 0)
-        s2(0)
-        q_mul(6, 1)
-        x_copy(2, "act")
-        r_mul(2, 1)
-        q_turn(7, 0)
-        phi(0, 0)
         q_quant(5)
-        q_turn(7, 1)
+        w_copy(("wx",), wx_raw, "act")
+        x_turn(2)
+        w_quant(("wphi", 0))
+        q_turn(3, 0)
+        r_quant(0)
+        r_mul(1, 1)
+        q_turn(3, 1)
+        q_mul(3, 0)
+        x_turn(3)
+        q_mul(3, 1)
+        s1(2, 1)
+        x_copy(2, "act")
+        w_quant(("wx",))
+        x_copy(3, "act")
+        r_quant(1)
+        s2(0)
+        q_quant(3)
+        x_quant(1)
+        q_turn(6, 0)
+        phi(0, 0)
+        r_mul(2, 1)
+        q_turn(6, 1)
         phi(0, 1)
-        q_quant(6)
+        q_mul(6, 0)
         s2(1)
         phi(0, 2)
-        q_mul(7, 0)
+        q_mul(6, 1)
         phi(0, 3)
-        x_turn(3)
-        q_mul(7, 1)
-        phi(1, 0)
         mix(0, 0)
-        s1(3, 0)
-        phi(1, 1)
+        q_turn(7, 0)
+        phi(1, 0)
         mix(0, 1)
         res_store(0, 0)
-        phi(1, 2)
+        q_turn(7, 1)
+        phi(1, 1)
+        q_mul(7, 0)
+        s1(3, 0)
+        o_cast(0, 0, "act")
+        q_mul(7, 1)
+        r_quant(2)
         mix(0, 2)
         s1(3, 1)
+        phi(1, 2)
+        mix(1, 0)
         phi(1, 3)
         mix(0, 3)
         res_store(0, 1)
-        x_copy(3, "act")
-        q_quant(7)
-        o_cast(0, 0, "act")
-        x_quant(1)
-        r_quant(2)
-        o_cast(0, 1, "act")
-        mix(1, 0)
         o_turn(0, 0)
+        q_quant(6)
+        o_cast(0, 1, "act")
+        s2(2)
         mix(1, 1)
         res_store(1, 0)
-        s2(2)
+        r_mul(3, 0)
         o_copy(0, 0, "act")
-        mix(1, 2)
         o_turn(0, 1)
+        r_mul(3, 1)
+        phi(2, 0)
+        s1(4, 0)
+        q_quant(7)
+        o_cast(1, 0, "act")
+        r_quant(3)
+        mix(1, 2)
+        phi(2, 1)
+        s1(4, 1)
+        mix(2, 0)
+        phi(2, 2)
         mix(1, 3)
         res_store(1, 1)
-        phi(2, 0)
-        r_mul(3, 0)
-        phi(2, 1)
-        r_mul(3, 1)
-        s1(4, 0)
-        phi(2, 2)
-        o_cast(1, 0, "dve")
-        phi(2, 3)
-        r_quant(3)
-        o_cast(1, 1, "act")
-        mix(2, 0)
-        s1(4, 1)
+        o_copy(0, 1, "act")
+        o_turn(1, 0)
         mix(2, 1)
         res_store(2, 0)
-        o_copy(0, 1, "act")
-        mix(2, 2)
-        s2(3)
-        o_cast(2, 0, "act")
-        mix(2, 3)
-        res_store(2, 1)
-        o_turn(1, 0)
+        o_cast(1, 1, "act")
         r_mul(4, 0)
-        o_turn(1, 1)
-        phi(3, 0)
+        s2(3)
         r_mul(4, 1)
+        phi(2, 3)
         s1(5, 0)
-        phi(3, 1)
         o_quant(0)
         o_store(0)
-        phi(3, 2)
+        phi(3, 0)
         r_quant(4)
-        phi(3, 3)
+        phi(3, 1)
+        o_cast(2, 0, "dve")
+        o_turn(1, 1)
+        o_copy(1, 0, "act")
+        mix(2, 2)
         s1(5, 1)
+        phi(3, 2)
         mix(3, 0)
-        o_cast(2, 1, "act")
-        r_mul(5, 0)
+        phi(3, 3)
+        mix(2, 3)
+        res_store(2, 1)
+        o_copy(1, 1, "act")
+        o_turn(2, 0)
         mix(3, 1)
         res_store(3, 0)
+        o_cast(2, 1, "act")
         s2(4)
-        o_copy(1, 0, "act")
-        mix(3, 2)
-        s1(6, 0)
-        o_copy(1, 1, "act")
-        mix(3, 3)
-        res_store(3, 1)
-        phi(4, 0)
+        r_mul(5, 0)
         r_mul(5, 1)
+        s1(6, 0)
+        o_copy(2, 0, "act")
+        o_cast(3, 0, "dve")
+        phi(4, 0)
+        r_quant(5)
+        mix(3, 2)
         phi(4, 1)
-        o_turn(2, 0)
+        o_turn(2, 1)
         o_quant(1)
         o_store(1)
-        o_turn(2, 1)
         phi(4, 2)
-        s1(6, 1)
-        r_quant(5)
-        r_mul(6, 0)
+        o_turn(3, 0)
         phi(4, 3)
         mix(4, 0)
-        o_cast(3, 0, "act")
-        s2(5)
+        s1(6, 1)
+        o_copy(2, 1, "act")
+        mix(3, 3)
+        res_store(3, 1)
+        o_copy(3, 0, "act")
         mix(4, 1)
         res_store(4, 0)
+        s2(5)
         o_cast(3, 1, "act")
-        mix(4, 2)
-        s1(7, 0)
-        mix(4, 3)
-        res_store(4, 1)
-        phi(5, 0)
+        r_mul(6, 0)
         r_mul(6, 1)
-        phi(5, 1)
-        o_cast(4, 0, "dve")
-        s1(7, 1)
-        phi(5, 2)
+        s1(7, 0)
+        phi(5, 0)
+        mix(4, 2)
+        o_cast(4, 0, "act")
         r_quant(6)
-        o_cast(4, 1, "dve")
-        phi(5, 3)
-        s2(6)
-        r_mul(7, 0)
-        o_copy(2, 0, "act")
-        mix(5, 0)
-        o_copy(2, 1, "act")
-        o_turn(3, 0)
-        mix(5, 1)
-        res_store(5, 0)
-        phi(6, 0)
         o_turn(3, 1)
         o_quant(2)
         o_store(2)
-        phi(6, 1)
-        mix(5, 2)
-        phi(6, 2)
-        mix(5, 3)
-        res_store(5, 1)
-        phi(6, 3)
-        r_mul(7, 1)
-        o_copy(3, 0, "act")
-        o_cast(5, 0, "dve")
+        s1(7, 1)
+        mix(5, 0)
+        phi(5, 1)
+        mix(4, 3)
+        res_store(4, 1)
+        phi(5, 2)
+        mix(5, 1)
+        res_store(5, 0)
         o_copy(3, 1, "act")
         o_turn(4, 0)
-        r_quant(7)
-        o_cast(5, 1, "act")
-        o_turn(4, 1)
+        r_mul(7, 0)
+        o_cast(4, 1, "act")
+        s2(6)
+        r_mul(7, 1)
         o_quant(3)
         o_store(3)
         scale_store(0)
+        phi(5, 3)
+        o_turn(4, 1)
+        phi(6, 0)
+        o_cast(5, 0, "dve")
+        o_copy(4, 0, "act")
+        r_quant(7)
+        mix(5, 2)
+        phi(6, 1)
         s2(7)
         mix(6, 0)
-        o_copy(4, 0, "act")
+        phi(6, 2)
+        mix(5, 3)
+        res_store(5, 1)
+        o_turn(5, 0)
+        phi(6, 3)
+        o_copy(4, 1, "dve")
+        phi(7, 0)
         mix(6, 1)
         res_store(6, 0)
-        o_copy(4, 1, "act")
-        o_turn(5, 0)
-        mix(6, 2)
-        phi(7, 0)
-        o_turn(5, 1)
-        mix(6, 3)
-        res_store(6, 1)
+        o_copy(5, 0, "act")
+        o_cast(5, 1, "dve")
         phi(7, 1)
         o_quant(4)
         o_store(4)
-        phi(7, 2)
-        o_cast(6, 0, "dve")
-        phi(7, 3)
+        o_cast(6, 0, "act")
+        o_turn(5, 1)
+        mix(6, 2)
         mix(7, 0)
-        o_cast(6, 1, "act")
+        phi(7, 2)
+        o_turn(6, 0)
+        mix(6, 3)
+        res_store(6, 1)
+        o_copy(5, 1, "act")
+        o_cast(7, 0, "dve", 0, 1)
+        phi(7, 3)
         mix(7, 1)
         res_store(7, 0)
-        mix(7, 2)
-        o_copy(5, 0, "act")
-        mix(7, 3)
-        res_store(7, 1)
-        o_copy(5, 1, "act")
-        o_turn(6, 0)
-        o_cast(7, 0, "dve", 0, 128)
-        o_turn(6, 1)
-        o_copy(6, 0, "act")
-        o_cast(7, 0, "dve", 128, 256)
-        o_cast(7, 1, "dve", 0, 128)
-        o_copy(6, 1, "act")
-        o_turn(7, 0)
-        o_cast(7, 1, "dve", 128, 256)
+        o_cast(6, 1, "act")
         o_quant(5)
         o_store(5)
-        o_turn(7, 1)
+        o_cast(7, 0, "dve", 1, 2)
+        o_copy(6, 0, "act")
+        mix(7, 2)
+        o_turn(6, 1)
+        mix(7, 3)
+        res_store(7, 1)
+        o_turn(7, 0)
+        o_copy(6, 1, "act")
+        o_cast(7, 1, "dve", 0, 1)
+        o_cast(7, 1, "dve", 1, 2)
+        o_copy(7, 0, "act")
         o_quant(6)
         o_store(6)
-        o_copy(7, 0, "act")
-        o_copy(7, 1, "act")
+        o_turn(7, 1)
         o_quant(7, 0, 1)
         o_store(7, 0, 1)
+        o_copy(7, 1, "dve")
         o_quant(7, 1, 2)
         o_store(7, 1, 2)
         scale_store(1)

from contextlib import ExitStack

import concourse.mybir as mybir
from concourse.masks import make_identity

N, D, S, R = 1024, 512, 512, 1024
ALPHA = (0.1, 0.3, 0.6, 0.8)
A = len(ALPHA)
C = A * S
FLOPS = 2 * N * (C * R + R * S + D * S)

P = 128
PACK = 4
KP = P * PACK
G1 = C // KP
G2 = R // KP
NT = N // P

F32 = mybir.dt.float32
BF16 = mybir.dt.bfloat16
U32 = mybir.dt.uint32
I32 = mybir.dt.int32
U8 = mybir.dt.uint8
FP8X4 = mybir.dt.float8_e4m3fn_x4
ALU = mybir.AluOpType
ACTF = mybir.ActivationFunctionType


def tile_statisticalrecurrentunitmultiscale_x1_kernel(
    tc, x, mu, gmu, wr, gr, wphi, wx, out_0, out_1, out_2
):
    nc = tc.nc
    with ExitStack() as ctx:
        ctx.enter_context(nc.allow_non_contiguous_dma(reason="two small gate vectors"))
        keep = ctx.enter_context(tc.tile_pool(name="keep", bufs=1))
        work = ctx.enter_context(tc.tile_pool(name="work", bufs=2))
        psum = ctx.enter_context(tc.psum_pool(name="psum", bufs=2))

        ctx.enter_context(tc.manual_schedule())

        gate_rows = keep.tile([P, KP], BF16, name="gate_rows", align_bytes=64)
        gate_perm = keep.tile([P, PACK, P], BF16, name="gate_perm", align_bytes=64)
        gmu_t = keep.tile([P, G1, PACK], BF16, name="gmu_t")
        gr_t = keep.tile([P, G2, PACK], BF16, name="gr_t")
        ident_bf = keep.tile([P, P], BF16, name="ident_bf")
        mu_sb = [keep.tile([P, C], BF16, name=f"mu_{i}", align_bytes=64) for i in range(NT)]
        x_sb = keep.tile([P, NT, D], BF16, name="x_sb", align_bytes=64)
        wr_raw = {
            (g, h): work.tile([P, PACK, KP], BF16, name=f"wr_raw_{g}_{h}", tag="big", bufs=8, align_bytes=64)
            for g in range(G1)
            for h in range(2)
        }
        wx_raw = keep.tile([P, PACK, S], BF16, name="wx_raw", align_bytes=64)
        wphi_raw = [keep.tile([P, PACK, S], BF16, name=f"wphi_raw_{g}", align_bytes=64) for g in range(G2)]

        def load_mu(i):
            nc.sync.dma_start(out=mu_sb[i][:], in_=mu[P * i : P * (i + 1), :])

        def load_wr(g, h):
            src = wr[KP * g : KP * (g + 1), :].rearrange("(p j) c -> p j c", j=PACK)
            nc.sync.dma_start(out=wr_raw[g, h][:], in_=src[:, :, KP * h : KP * (h + 1)])

        def load_x():
            nc.sync.dma_start(out=x_sb[:], in_=x.rearrange("(i p) d -> p i d", p=P))

        def load_wx():
            nc.sync.dma_start(out=wx_raw[:], in_=wx.rearrange("(p j) c -> p j c", j=PACK))

        def load_wphi(g):
            src = wphi[KP * g : KP * (g + 1), :].rearrange("(s t v) c -> v s t c", t=PACK, v=2)
            for v in range(2):
                nc.sync.dma_start(out=wphi_raw[g][v:P:2, :, :], in_=src[v])

        nc.vector.memset(gate_rows[:], 0.0)

        def load_gates():
            nc.sync.dma_start(out=gate_rows[0:G1, :], in_=gmu.rearrange("(g c) -> g c", g=G1))
            nc.sync.dma_start(out=gate_rows[G1 : G1 + G2, :], in_=gr.rearrange("(g c) -> g c", g=G2))

        load_wr(3, 0)
        load_gates()
        load_wr(1, 1)
        load_wr(1, 0)
        load_mu(1)
        load_wr(2, 0)
        load_mu(2)
        load_wr(0, 0)
        load_mu(0)
        load_wphi(1)
        load_wr(0, 1)
        load_wr(2, 1)
        load_mu(4)
        load_wr(3, 1)
        load_x()
        load_mu(5)
        load_wphi(0)
        load_wx()
        load_mu(7)
        load_mu(3)
        load_mu(6)

        ident = keep.tile([P, P], F32, name="ident")
        make_identity(nc, ident[:])
        warm = keep.tile([P, 1], F32, name="warm")
        nc.vector.memset(warm[:], 0.0)
        nc.scalar.activation(out=warm[:], in_=warm[:], func=ACTF.Relu)

        gate_ps = psum.tile([P, 2, P], F32, name="gate_ps", tag="y_ps", bufs=2)
        for u in range(2):
            nc.tensor.transpose(gate_ps[:, u, :], gate_rows[:].bitcast(F32)[:, u : KP // 2 : 2], ident[:])
        nc.scalar.copy(
            out=gmu_t[:].rearrange("p g t -> p (g t)").bitcast(F32).rearrange("p (g u) -> p g u", u=2),
            in_=gate_ps[:, :, 0:G1].rearrange("p u g -> p g u"),
        )
        make_identity(nc, ident_bf[:])
        nc.gpsimd.tensor_copy(
            out=gate_perm[:].rearrange("p t (s v) -> p t s v", v=2),
            in_=gate_rows[:].rearrange("p (s t v) -> p t s v", t=PACK, v=2),
        )

        def gr_turn():
            ps = psum.tile([P, PACK, P], BF16, name="gr_ps", tag="y_ps", bufs=2)
            for t in range(PACK):
                nc.tensor.transpose(ps[:, t, :], gate_perm[:, t, :], ident_bf[:])
            nc.scalar.copy(out=gr_t[:], in_=ps[:, :, G1 : G1 + G2].rearrange("p t g -> p g t"))


        codes, scales, grouped = {}, {}, {}

        def copy_on(engine, out, in_):
            if engine == "act":
                nc.scalar.copy(out=out, in_=in_)
            else:
                nc.vector.tensor_copy(out=out, in_=in_)

        def wr_copy(g, h, engine):
            gt = work.tile([P, PACK, P, PACK], BF16, name="w_grouped", tag="w_grouped", bufs=4, align_bytes=64)
            grouped["wr", g, h] = gt
            copy_on(
                engine,
                gt[:].rearrange("p t (s v) j -> p s t v j", v=2),
                wr_raw[g, h][:].rearrange("p j (s t v) -> p s t v j", t=PACK, v=2),
            )

        def w_copy(key, raw, engine):
            gt = work.tile([P, S, PACK], BF16, name="w_grouped", tag="w_grouped", bufs=4, align_bytes=64)
            grouped[key] = gt
            copy_on(engine, gt[:], raw[:].rearrange("p j c -> p c j"))

        def w_quant(key):
            nm = "_".join(str(k) for k in key)
            ct = keep.tile([P, KP], U32, name="wc_" + nm, align_bytes=64)
            st = keep.tile([P, KP], U8, name="ws_" + nm, align_bytes=64)
            codes[key], scales[key] = ct, st
            src = grouped[key][:]
            src = src.rearrange("p t m j -> p (t m j)") if key[0] == "wr" else src.rearrange("p c j -> p (c j)")
            nc.vector.quantize_mx(out=ct[:].bitcast(FP8X4), scales=st[:], in_=src)

        q_ps, q_gr, q_codes, q_scales = {}, {}, {}, {}

        def q_turn(i, b):
            words = mu_sb[i][:].bitcast(F32)
            ps = psum.tile([P, 2, 2, P], F32, name="q_ps", tag="q_ps", bufs=2)
            q_ps[i, b] = ps
            for k in range(2):
                g = 2 * b + k
                for u in range(2):
                    nc.tensor.transpose(ps[:, u, k, :], words[:, 256 * g + u : 256 * (g + 1) : 2], ident[:])

        def q_mul(i, b):
            if i not in q_gr:
                q_gr[i] = work.tile([P, G1, P, 2, 2], BF16, name="q_gr", tag="q_gr", bufs=2, align_bytes=64)
            src = q_ps[i, b][:].rearrange("p u g r -> p u (g r)").bitcast(BF16)
            nc.vector.tensor_tensor(
                out=q_gr[i][:, 2 * b : 2 * b + 2],
                in0=src.rearrange("p u (g r e) -> p g r u e", g=2, e=2),
                in1=gmu_t[:, 2 * b : 2 * b + 2].rearrange("p g (u e) -> p g u e", e=2).unsqueeze(2).to_broadcast([P, 2, P, 2, 2]),
                op=ALU.mult,
            )

        def q_quant(i):
            ct = work.tile([P, G1, P], U32, name="q_codes", tag="q_codes", bufs=8, align_bytes=64)
            st = work.tile([P, G1, P], U8, name="q_scales", tag="q_scales", bufs=8, align_bytes=64)
            q_codes[i], q_scales[i] = ct, st
            nc.vector.quantize_mx(
                out=ct[:].rearrange("p g n -> p (g n)").bitcast(FP8X4),
                scales=st[:].rearrange("p g n -> p (g n)"),
                in_=q_gr[i][:].rearrange("p g n u e -> p (g n u e)"),
            )

        x_gr = keep.tile([P, N, PACK], BF16, name="x_gr", align_bytes=64)
        x_codes = keep.tile([P, N], U32, name="x_codes", align_bytes=64)
        x_scales = keep.tile([P, N], U8, name="x_scales", align_bytes=64)
        x_ps = {}

        def x_turn(j):
            ps = psum.tile([P, 2, 2, P], F32, name="o_ps", tag="o_ps", bufs=2)
            x_ps[j] = ps
            for k in range(2):
                words = x_sb[:, 2 * j + k, :].bitcast(F32)
                for u in range(2):
                    nc.tensor.transpose(ps[:, u, k, :], words[:, u : 256 : 2], ident[:])

        def x_copy(j, engine):
            copy_on(
                engine,
                x_gr[:, 256 * j : 256 * (j + 1), :].rearrange("p n t -> p (n t)").bitcast(F32).rearrange("p (n u) -> p n u", u=2),
                x_ps[j][:].rearrange("p u k r -> p (k r) u"),
            )

        def x_quant(h):
            w = N // 2
            nc.vector.quantize_mx(
                out=x_codes[:, w * h : w * (h + 1)].bitcast(FP8X4),
                scales=x_scales[:, w * h : w * (h + 1)],
                in_=x_gr[:, w * h : w * (h + 1), :].rearrange("p n t -> p (n t)"),
            )

        z_ps, r_gr, r_codes, r_scales = {}, {}, {}, {}

        def s1(i, h):
            ps = psum.tile([P, PACK, P], F32, name="z_ps", tag="z_ps", bufs=2)
            z_ps[i, h] = ps
            for t in range(PACK):
                cols = slice(P * t, P * (t + 1))
                for g in range(G1):
                    nc.tensor.matmul_mx(
                        out=ps[:, t, :],
                        lhsT=codes["wr", g, h][:, cols].bitcast(FP8X4),
                        lhsT_scale=scales["wr", g, h][:, cols],
                        rhs=q_codes[i][:, g, :].bitcast(FP8X4),
                        rhs_scale=q_scales[i][:, g, :],
                        start=(g == 0),
                        stop=(g == G1 - 1),
                    )

        def r_mul(i, h):
            if i not in r_gr:
                r_gr[i] = work.tile([P, G2, P, PACK], BF16, name="r_gr", tag="r_gr", bufs=3, align_bytes=64)
            nc.vector.scalar_tensor_tensor(
                out=r_gr[i][:, h],
                in0=z_ps[i, h][:].rearrange("p t n -> p n t"),
                scalar=0.0,
                in1=gr_t[:, h, :].unsqueeze(1).to_broadcast([P, P, PACK]),
                op0=ALU.max,
                op1=ALU.mult,
            )

        def r_quant(i):
            ct = work.tile([P, G2, P], U32, name="r_codes", tag="r_codes", bufs=4, align_bytes=64)
            st = work.tile([P, G2, P], U8, name="r_scales", tag="r_scales", bufs=4, align_bytes=64)
            r_codes[i], r_scales[i] = ct, st
            nc.vector.quantize_mx(
                out=ct[:].rearrange("p g n -> p (g n)").bitcast(FP8X4),
                scales=st[:].rearrange("p g n -> p (g n)"),
                in_=r_gr[i][:].rearrange("p g n t -> p (g n t)"),
            )

        y_ps, part, res = {}, {}, {}

        def s2(i):
            ps = psum.tile([P, S], F32, name="y_ps", tag="y_ps", bufs=2)
            y_ps[i] = ps
            rows = slice(P * i, P * (i + 1))
            nc.tensor.matmul_mx(
                out=ps[:],
                lhsT=x_codes[:, rows].bitcast(FP8X4),
                lhsT_scale=x_scales[:, rows],
                rhs=codes["wx",][:].bitcast(FP8X4),
                rhs_scale=scales["wx",][:],
                start=True,
                stop=False,
            )
            for g in range(G2):
                nc.tensor.matmul_mx(
                    out=ps[:],
                    lhsT=r_codes[i][:, g, :].bitcast(FP8X4),
                    lhsT_scale=r_scales[i][:, g, :],
                    rhs=codes["wphi", g][:].bitcast(FP8X4),
                    rhs_scale=scales["wphi", g][:],
                    start=False,
                    stop=(g == G2 - 1),
                )

        def phi(i, a):
            pt = work.tile([P, S], F32, name="part", tag="part", bufs=6)
            part[i, a] = pt
            nc.scalar.activation(out=pt[:], in_=y_ps[i][:], func=ACTF.Relu, scale=1.0 - ALPHA[a])

        def mix(i, a):
            b, k = a // 2, a % 2
            if (i, b) not in res:
                res[i, b] = work.tile([P, C // 2], F32, name="res", tag="big", bufs=8, align_bytes=64)
            nc.vector.scalar_tensor_tensor(
                out=res[i, b][:, S * k : S * (k + 1)],
                in0=mu_sb[i][:, S * a : S * (a + 1)],
                scalar=ALPHA[a],
                in1=part[i, a][:],
                op0=ALU.mult,
                op1=ALU.add,
            )

        def res_store(i, b):
            w = C // 2
            nc.sync.dma_start(out=out_0[P * i : P * (i + 1), w * b : w * (b + 1)], in_=res[i, b][:])

        o_bf, o_ps, o_gr, o_codes, o_scales = {}, {}, {}, {}, {}

        def o_cast(i, b, engine, k0=0, k1=2):
            if (i, b) not in o_bf:
                o_bf[i, b] = work.tile([P, C // 2], BF16, name="o_bf", tag="o_bf", bufs=4, align_bytes=64)
            cols = slice(S * k0, S * k1)
            copy_on(engine, o_bf[i, b][:, cols], res[i, b][:, cols])

        def o_turn(i, b):
            ps = psum.tile([P, 2, 2, P], F32, name="o_ps", tag="o_ps", bufs=2)
            o_ps[i, b] = ps
            words = o_bf[i, b][:].bitcast(F32)
            for k in range(2):
                for u in range(2):
                    nc.tensor.transpose(ps[:, u, k, :], words[:, 256 * k + u : 256 * (k + 1) : 2], ident[:])

        def o_copy(i, b, engine="act"):
            if i not in o_gr:
                o_gr[i] = work.tile([P, G1, P, PACK], BF16, name="o_gr", tag="o_gr", bufs=2, align_bytes=64)
            copy_on(
                engine,
                o_gr[i][:, 2 * b : 2 * b + 2].rearrange("p g n t -> p (g n t)").bitcast(F32).rearrange("p (n u) -> p n u", u=2),
                o_ps[i, b][:].rearrange("p u k r -> p (k r) u"),
            )

        scales_half = [keep.tile([P, G1, N // 2], U8, name=f"o_scales_{k}", align_bytes=64) for k in range(2)]

        def o_quant(i, b0=0, b1=2):
            if i not in o_codes:
                o_codes[i] = work.tile([P, G1, P], U32, name="o_codes", tag="o_codes", bufs=3, align_bytes=64)
            for g in range(2 * b0, 2 * b1):
                nc.vector.quantize_mx(
                    out=o_codes[i][:, g, :].bitcast(FP8X4),
                    scales=scales_half[i // 4][:, g, P * (i % 4) : P * (i % 4 + 1)],
                    in_=o_gr[i][:, g].rearrange("p n t -> p (n t)"),
                )

        def o_store(i, b0=0, b1=2):
            gs = slice(2 * b0, 2 * b1)
            words = out_1.rearrange("g p m t -> p g (m t)")
            nc.sync.dma_start(
                out=words[:, gs, KP * i : KP * (i + 1)].bitcast(I32), in_=o_codes[i][:, gs].bitcast(I32)
            )

        def scale_store(k):
            w = N // 2
            rows = out_2.rearrange("g (q r) m -> q r g m", r=4)
            for q in range(4):
                nc.sync.dma_start(
                    out=rows[q, :, :, w * k : w * (k + 1)].bitcast(I32),
                    in_=scales_half[k][32 * q : 32 * q + 4].bitcast(I32),
                )

        wr_copy(3, 0, "dve")
        wr_copy(1, 1, "act")
        w_quant(("wr", 3, 0))
        wr_copy(1, 0, "dve")
        q_turn(1, 0)
        w_quant(("wr", 1, 1))
        q_turn(1, 1)
        q_mul(1, 0)
        wr_copy(2, 0, "act")
        w_quant(("wr", 1, 0))
        q_mul(1, 1)
        q_turn(2, 0)
        q_quant(1)
        q_turn(2, 1)
        q_mul(2, 0)
        wr_copy(0, 0, "act")
        q_mul(2, 1)
        w_quant(("wr", 2, 0))
        q_turn(0, 0)
        q_quant(2)
        q_turn(0, 1)
        q_mul(0, 0)
        q_mul(0, 1)
        w_copy(("wphi", 1), wphi_raw[1], "act")
        w_quant(("wr", 0, 0))
        wr_copy(0, 1, "dve")
        s1(1, 0)
        q_quant(0)
        wr_copy(2, 1, "act")
        s1(2, 0)
        w_quant(("wr", 0, 1))
        w_quant(("wphi", 1))
        q_turn(4, 0)
        gr_turn()
        r_mul(1, 0)
        q_turn(4, 1)
        r_mul(2, 0)
        wr_copy(3, 1, "act")
        s1(0, 0)
        w_quant(("wr", 2, 1))
        q_mul(4, 0)
        q_mul(4, 1)
        x_turn(0)
        r_mul(0, 0)
        x_turn(1)
        q_quant(4)
        x_copy(0, "act")
        q_turn(5, 0)
        w_quant(("wr", 3, 1))
        x_copy(1, "act")
        q_turn(5, 1)
        q_mul(5, 0)
        w_copy(("wphi", 0), wphi_raw[0], "act")
        s1(0, 1)
        x_quant(0)
        q_mul(5, 1)
        s1(1, 1)
        r_mul(0, 1)
        q_quant(5)
        w_copy(("wx",), wx_raw, "act")
        x_turn(2)
        w_quant(("wphi", 0))
        q_turn(3, 0)
        r_quant(0)
        r_mul(1, 1)
        q_turn(3, 1)
        q_mul(3, 0)
        x_turn(3)
        q_mul(3, 1)
        s1(2, 1)
        x_copy(2, "act")
        w_quant(("wx",))
        x_copy(3, "act")
        r_quant(1)
        s2(0)
        q_quant(3)
        x_quant(1)
        q_turn(6, 0)
        phi(0, 0)
        r_mul(2, 1)
        q_turn(6, 1)
        phi(0, 1)
        q_mul(6, 0)
        s2(1)
        phi(0, 2)
        q_mul(6, 1)
        phi(0, 3)
        mix(0, 0)
        q_turn(7, 0)
        phi(1, 0)
        mix(0, 1)
        res_store(0, 0)
        q_turn(7, 1)
        phi(1, 1)
        q_mul(7, 0)
        s1(3, 0)
        o_cast(0, 0, "act")
        q_mul(7, 1)
        r_quant(2)
        mix(0, 2)
        s1(3, 1)
        phi(1, 2)
        mix(1, 0)
        phi(1, 3)
        mix(0, 3)
        res_store(0, 1)
        o_turn(0, 0)
        q_quant(6)
        o_cast(0, 1, "act")
        s2(2)
        mix(1, 1)
        res_store(1, 0)
        r_mul(3, 0)
        o_copy(0, 0, "act")
        o_turn(0, 1)
        r_mul(3, 1)
        phi(2, 0)
        s1(4, 0)
        q_quant(7)
        o_cast(1, 0, "act")
        r_quant(3)
        mix(1, 2)
        phi(2, 1)
        s1(4, 1)
        mix(2, 0)
        phi(2, 2)
        mix(1, 3)
        res_store(1, 1)
        o_copy(0, 1, "act")
        o_turn(1, 0)
        mix(2, 1)
        res_store(2, 0)
        o_cast(1, 1, "act")
        r_mul(4, 0)
        s2(3)
        r_mul(4, 1)
        phi(2, 3)
        s1(5, 0)
        o_quant(0)
        o_store(0)
        phi(3, 0)
        r_quant(4)
        phi(3, 1)
        o_cast(2, 0, "dve")
        o_turn(1, 1)
        o_copy(1, 0, "act")
        mix(2, 2)
        s1(5, 1)
        phi(3, 2)
        mix(3, 0)
        phi(3, 3)
        mix(2, 3)
        res_store(2, 1)
        o_copy(1, 1, "act")
        o_turn(2, 0)
        mix(3, 1)
        res_store(3, 0)
        o_cast(2, 1, "act")
        s2(4)
        r_mul(5, 0)
        r_mul(5, 1)
        s1(6, 0)
        o_copy(2, 0, "act")
        o_cast(3, 0, "dve")
        phi(4, 0)
        r_quant(5)
        mix(3, 2)
        phi(4, 1)
        o_turn(2, 1)
        o_quant(1)
        o_store(1)
        phi(4, 2)
        o_turn(3, 0)
        phi(4, 3)
        mix(4, 0)
        s1(6, 1)
        o_copy(2, 1, "act")
        mix(3, 3)
        res_store(3, 1)
        o_copy(3, 0, "act")
        mix(4, 1)
        res_store(4, 0)
        s2(5)
        o_cast(3, 1, "act")
        r_mul(6, 0)
        r_mul(6, 1)
        s1(7, 0)
        phi(5, 0)
        mix(4, 2)
        o_cast(4, 0, "act")
        r_quant(6)
        o_turn(3, 1)
        o_quant(2)
        o_store(2)
        s1(7, 1)
        mix(5, 0)
        phi(5, 1)
        mix(4, 3)
        res_store(4, 1)
        phi(5, 2)
        mix(5, 1)
        res_store(5, 0)
        o_copy(3, 1, "act")
        o_turn(4, 0)
        r_mul(7, 0)
        o_cast(4, 1, "act")
        s2(6)
        r_mul(7, 1)
        o_quant(3)
        o_store(3)
        scale_store(0)
        phi(5, 3)
        o_turn(4, 1)
        phi(6, 0)
        o_cast(5, 0, "dve")
        o_copy(4, 0, "act")
        r_quant(7)
        mix(5, 2)
        phi(6, 1)
        s2(7)
        mix(6, 0)
        phi(6, 2)
        mix(5, 3)
        res_store(5, 1)
        o_turn(5, 0)
        phi(6, 3)
        o_copy(4, 1, "dve")
        phi(7, 0)
        mix(6, 1)
        res_store(6, 0)
        o_copy(5, 0, "act")
        o_cast(5, 1, "dve")
        phi(7, 1)
        o_quant(4)
        o_store(4)
        o_cast(6, 0, "act")
        o_turn(5, 1)
        mix(6, 2)
        mix(7, 0)
        phi(7, 2)
        o_turn(6, 0)
        mix(6, 3)
        res_store(6, 1)
        o_copy(5, 1, "act")
        o_cast(7, 0, "dve", 0, 1)
        phi(7, 3)
        mix(7, 1)
        res_store(7, 0)
        o_cast(6, 1, "act")
        o_quant(5)
        o_store(5)
        o_cast(7, 0, "dve", 1, 2)
        o_copy(6, 0, "act")
        mix(7, 2)
        o_turn(6, 1)
        mix(7, 3)
        res_store(7, 1)
        o_turn(7, 0)
        o_copy(6, 1, "act")
        o_cast(7, 1, "dve", 0, 1)
        o_cast(7, 1, "dve", 1, 2)
        o_copy(7, 0, "act")
        o_quant(6)
        o_store(6)
        o_turn(7, 1)
        o_quant(7, 0, 1)
        o_store(7, 0, 1)
        o_copy(7, 1, "dve")
        o_quant(7, 1, 2)
        o_store(7, 1, 2)
        scale_store(1)
